import numpy as np
import ml_dtypes


def mxq(x, axis, fmt="e4m3"):
    dtype, down = {"e4m3": (ml_dtypes.float8_e4m3fn, 7), "e5m2": (ml_dtypes.float8_e5m2, 14)}[fmt]
    v = np.moveaxis(np.asarray(x, np.float32).astype(ml_dtypes.bfloat16).astype(np.float64), axis, -1)
    blocks = v.reshape(v.shape[:-1] + (-1, 32))
    amax = np.abs(blocks).max(-1, keepdims=True)
    byte = np.maximum(np.where(amax > 0, np.frexp(amax)[1] - 1 + 127, 0) - down, 1)
    scale = np.exp2(byte - 127.0)
    codes = (blocks / scale).astype(np.float32).astype(dtype).astype(np.float64)
    return np.moveaxis((codes * scale).reshape(v.shape), -1, axis)


WIDE = False


def mx_kscale(k):
    if not WIDE:
        return np.ones(k)
    levels = np.array([10, -10, 5, -5, 0])
    if k % 512:
        return np.exp2(np.random.permutation(np.resize(levels, k // 32))).repeat(32)
    a = np.empty((k // 512, 16))
    for p in range(k // 512):
        a[p, :8] = np.random.permutation(np.resize(levels, 8))
        for g in range(8):
            far = levels[np.abs(levels - a[p, g]) >= 10]
            a[p, g + 8] = far[np.random.randint(len(far))]
    return np.exp2(a.ravel()).repeat(32)


def f64(x):
    return np.asarray(x).astype(np.float64)


def striped8(idx):
    return np.concatenate([x.reshape(-1, 16).T for x in idx]).astype(np.uint16)


def runs(offs, k):
    lists = np.stack([offs[16 * r : 16 * r + 16].T.reshape(-1) for r in range(8)]).astype(np.int64)
    return lists[np.arange(k) % 512 // 64]


def pack_weight(w):
    k, n = w.shape
    w = f64(np.asarray(w, np.float32).astype(ml_dtypes.bfloat16)).reshape(k // 32, 32, n)
    amax = np.abs(w).max(1)
    byte = np.clip(np.where(amax > 0, np.frexp(amax)[1] - 1 + 127 - 7, 1), 1, 254)
    scaled = (w * np.exp2(127.0 - byte)[:, None, :]).reshape(k, n).astype(np.float32)
    words = np.ascontiguousarray(scaled.reshape(k // 512, 128, 4, n).transpose(0, 1, 3, 2)).astype(ml_dtypes.float8_e4m3fn).view(np.uint8)
    return words, np.ascontiguousarray(byte.astype(np.uint8).reshape(k // 512, 16, n))


def unpack_weight(words, scales):
    g, p, n, _ = words.shape
    vals = np.ascontiguousarray(words).view(ml_dtypes.float8_e4m3fn).astype(np.float64) * np.repeat(np.exp2(scales.astype(np.float64) - 127.0), 8, axis=1)[..., None]
    return vals.transpose(0, 1, 3, 2).reshape(g * 512, n)


def gelu(v):
    return 0.5 * v * (1.0 + np.tanh(np.sqrt(2.0 / np.pi) * (v + 0.044715 * v**3)))


K, T, S, H, N = 512, 2048, 1024, 512, 256


def setup_inputs():
    n = np.random.standard_normal
    s = mx_kscale(K)[:, None]
    u = mx_kscale(H)
    packed_xT = pack_weight(n((K, T)) * s)
    packed_w2 = pack_weight(n((H, N)) / np.sqrt(H) / u[:, None])
    return {
        "x_words": packed_xT[0],
        "x_scales": packed_xT[1],
        "w1": (n((K, H)) / np.sqrt(K) / s * u).astype(np.float32),
        "w2_words": packed_w2[0],
        "w2_scales": packed_w2[1],
        "pos": (0.5 * n((H, S)) * u[:, None]).astype(np.float32),
        "offs": striped8(np.random.randint(0, T, (8, S))),
    }


def reference(x_words, x_scales, w1, w2_words, w2_scales, pos, offs):
    xq = unpack_weight(x_words, x_scales)[np.arange(K)[:, None], runs(offs, K)]
    h = gelu((mxq(f64(w1), 0, "e4m3").T @ xq) + f64(pos))
    return unpack_weight(w2_words, w2_scales).T @ mxq(h, 0, "e4m3")

@@ -1,0 +1,163 @@
+from contextlib import ExitStack
+
+import concourse.mybir as mybir
+
+K, T, S, H, N = 512, 2048, 1024, 512, 256
+FLOPS = 2 * K * H * S + 2 * H * N * S
+
+F32 = mybir.dt.float32
+BF16 = mybir.dt.bfloat16
+I32 = mybir.dt.int32
+U32 = mybir.dt.uint32
+U16 = mybir.dt.uint16
+U8 = mybir.dt.uint8
+FP8X4 = mybir.dt.float8_e4m3fn_x4
+GELU = mybir.ActivationFunctionType.Gelu_apprx_tanh
+ADD = mybir.AluOpType.add
+
+P = 128
+UNIT = 128
+GATHER = 256
+SCALE_PIECE = 512
+POS_CUTS = (0, 256, 512, 1024)
+OUT_WIDTHS = (256, 256, 256, 128, 128)
+
+
+def tile_picked_phpq_gelu_p_kernel(tc, x_words, x_scales, w1, w2_words, w2_scales, pos, offs, out):
+    nc = tc.nc
+    with ExitStack() as ctx:
+        held = ctx.enter_context(tc.tile_pool(name="held", bufs=1))
+        ring = ctx.enter_context(tc.tile_pool(name="ring", bufs=1))
+        reuse = ctx.enter_context(tc.tile_pool(name="reuse", bufs=1))
+        reuse_raw = ctx.enter_context(tc.tile_pool(name="reuse_raw", bufs=1))
+        psum = ctx.enter_context(tc.psum_pool(name="psum", bufs=1))
+
+        offsets = held.tile([P, S // 16], U16, name="offsets")
+        nc.sync.dma_start(offsets[:], offs)
+
+        scale_table = reuse.tile([P, T], U8, name="scale_table", align_bytes=64, offset=0)
+        nc.vector.memset(scale_table[:].bitcast(I32), 0)
+        rows_by_parity = x_scales[0].rearrange("(r e) c -> e r c", e=2)
+        for e in range(2):
+            nc.sync.dma_start(scale_table[e:P:16, :].bitcast(I32), rows_by_parity[e].bitcast(I32))
+
+        w1_rows = w1.rearrange("(p j) c -> p j c", j=4)
+        w1_raw = []
+        for half in range(2):
+            raw = reuse_raw.tile([P, 4, H // 2], F32, name="w1_raw%d" % half, tag="stage%d" % (half + 1))
+            nc.scalar.dma_start(raw[:], w1_rows[:, :, half * (H // 2) : (half + 1) * (H // 2)])
+            w1_raw.append(raw)
+        word_table = held.tile([P, T], U32, name="word_table", align_bytes=64)
+        nc.scalar.dma_start(word_table[:].bitcast(I32), x_words[0].rearrange("p c r -> p (c r)").bitcast(I32))
+        pos_rows = pos.rearrange("(p t) j -> p t j", t=4)
+        pos_parts = []
+
+        def load_pos(part):
+            lo, hi = POS_CUTS[part], POS_CUTS[part + 1]
+            piece = reuse_raw.tile([P, 4, hi - lo], F32, name="pos%d" % part, tag="stage%d" % part)
+            nc.scalar.dma_start(piece[:], pos_rows[:, :, lo:hi])
+            pos_parts.append((lo, hi, piece))
+
+        load_pos(0)
+
+        w2_plane = held.tile([P, N], U8, name="w2_plane", align_bytes=64)
+        nc.vector.memset(w2_plane[:].bitcast(I32), 0)
+        warm = held.tile([P, 2], F32, name="warm")
+        nc.vector.memset(warm[:, 0:1], 0.0)
+        nc.scalar.activation(warm[:, 1:2], warm[:, 0:1], GELU)
+        w2_codes = held.tile([P, N], U32, name="w2_codes", align_bytes=64)
+        nc.gpsimd.dma_start(w2_codes[:].bitcast(I32), w2_words[0].rearrange("p c r -> p (c r)").bitcast(I32))
+        for q in range(4):
+            nc.gpsimd.dma_start(w2_plane[32 * q : 32 * q + 4, :].bitcast(I32), w2_scales[0, 4 * q : 4 * q + 4, :].bitcast(I32))
+
+        x_planes = []
+        for piece in range(S // SCALE_PIECE):
+            picked = held.tile([P, SCALE_PIECE], U8, name="picked_scales%d" % piece, align_bytes=64)
+            plane = held.tile([P, SCALE_PIECE], U8, name="x_plane%d" % piece, align_bytes=64)
+            cols = slice(piece * SCALE_PIECE // 16, (piece + 1) * SCALE_PIECE // 16)
+            nc.vector.tensor_copy(picked[:], scale_table[:].indirect(offsets[:, cols]))
+            nc.vector.tensor_copy(plane[:].bitcast(I32), picked[:].bitcast(I32))
+            for e in range(2):
+                nc.sync.dma_start(plane[2 + e : P : 32, :].bitcast(I32), picked[16 + e : P : 32, :].bitcast(I32))
+            x_planes.append(plane)
+
+        w1_bf = held.tile([P, 4 * H], BF16, name="w1_bf", align_bytes=64)
+        w1_dealt = w1_bf[:].rearrange("p (t m j) -> p m j t", t=4, j=4)
+        for half in range(2):
+            nc.scalar.copy(w1_dealt[:, half * 64 : (half + 1) * 64], w1_raw[half][:].rearrange("p j (m t) -> p m j t", t=4))
+            load_pos(half + 1)
+        w1_codes = held.tile([P, H], U32, name="w1_codes", align_bytes=64)
+        w1_plane = reuse.tile([P, H], U8, name="w1_plane", align_bytes=64, offset=0)
+        nc.vector.quantize_mx(out=w1_codes[:].bitcast(FP8X4), scales=w1_plane[:], in_=w1_bf[:])
+
+        picked_words = {}
+        hidden = {}
+
+        def gather_words(g):
+            words = reuse.tile([P, GATHER], U32, name="picked_words", bufs=2, align_bytes=64, offset=H)
+            nc.vector.tensor_copy(words[:], word_table[:].indirect(offsets[:, g * GATHER // 16 : (g + 1) * GATHER // 16]))
+            picked_words[g] = words
+
+        starts = [sum(OUT_WIDTHS[:b]) for b in range(len(OUT_WIDTHS))]
+
+        def block_of(col):
+            return max(b for b in range(len(starts)) if starts[b] <= col)
+
+        def first_layer(u):
+            col = u * UNIT
+            words = picked_words[col // GATHER][:, col % GATHER : col % GATHER + UNIT]
+            plane = x_planes[col // SCALE_PIECE][:, col % SCALE_PIECE : col % SCALE_PIECE + UNIT]
+            acc = psum.tile([P, 4, UNIT], F32, name="acc", bufs=4)
+            for t in range(4):
+                nc.tensor.matmul_mx(
+                    out=acc[:, t, :],
+                    lhsT=w1_codes[:, t * P : (t + 1) * P].bitcast(FP8X4),
+                    lhsT_scale=w1_plane[:, t * P : (t + 1) * P],
+                    rhs=words.bitcast(FP8X4),
+                    rhs_scale=plane,
+                    start=True,
+                    stop=True,
+                )
+            lo, hi, piece = [part for part in pos_parts if part[0] <= col < part[1]][0]
+            pre = ring.tile([P, 4, UNIT], F32, name="pre", bufs=4)
+            nc.vector.tensor_tensor(pre[:], acc[:], piece[:, :, col - lo : col - lo + UNIT], ADD)
+            b = block_of(col)
+            if b not in hidden:
+                hidden[b] = ring.tile([P, 4 * OUT_WIDTHS[b]], BF16, name="hidden", bufs=3, align_bytes=64)
+            at = 4 * (col - starts[b])
+            nc.scalar.activation(
+                hidden[b][:, at : at + 4 * UNIT].rearrange("p (c i t) -> p c t i", i=4, t=4),
+                pre[:].rearrange("p t (c i) -> p c t i", i=4),
+                GELU,
+            )
+
+        def second_layer(b):
+            width = OUT_WIDTHS[b]
+            codes = ring.tile([P, width], U32, name="h_codes", bufs=3, align_bytes=64)
+            plane = ring.tile([P, width], U8, name="h_plane", bufs=3, align_bytes=64)
+            nc.vector.quantize_mx(out=codes[:].bitcast(FP8X4), scales=plane[:], in_=hidden[b][:])
+            res = psum.tile([P, 2, width], F32, name="res", bufs=3)
+            for m in range(2):
+                nc.tensor.matmul_mx(
+                    out=res[:, m, :],
+                    lhsT=w2_codes[:, m * P : (m + 1) * P].bitcast(FP8X4),
+                    lhsT_scale=w2_plane[:, m * P : (m + 1) * P],
+                    rhs=codes[:].bitcast(FP8X4),
+                    rhs_scale=plane[:],
+                    start=True,
+                    stop=True,
+                )
+            staged = ring.tile([P, 2, width], F32, name="staged", bufs=5)
+            nc.scalar.copy(staged[:], res[:])
+            nc.sync.dma_start(out.rearrange("(m p) j -> p m j", p=P)[:, :, starts[b] : starts[b] + width], staged[:])
+
+        done = 0
+        for u in range(S // UNIT):
+            if u * UNIT % GATHER == 0:
+                gather_words(u * UNIT // GATHER)
+            first_layer(u)
+            while done < len(OUT_WIDTHS) and starts[done] + OUT_WIDTHS[done] <= u * UNIT:
+                second_layer(done)
+                done = done + 1
+        for b in range(done, len(OUT_WIDTHS)):
+            second_layer(b)

@@ -16,11 +16,17 @@ GELU = mybir.ActivationFunctionType.Gelu_apprx_tanh
 ADD = mybir.AluOpType.add
 
 P = 128
-UNIT = 128
-GATHER = 256
-SCALE_PIECE = 512
-POS_CUTS = (0, 256, 512, 1024)
-OUT_WIDTHS = (256, 256, 256, 128, 128)
+WORD_CUTS = (0, 768, S)
+W1_CUTS = (0, 320, H)
+POS_CUTS = (0, 256, 512, S)
+ON_VECTOR = (2,)
+TABLE_AT = 8192
+W2_AT = TABLE_AT + 64
+POS_AT = TABLE_AT + 64 - 8192
+WORDS_AT = (9280, 16384)
+CAST_AT = 16384
+UNITS = (128, 128, 128, 128, 128, 128, 128, 128)
+BLOCKS = ((0, 2, 3), (2, 4, 5), (4, 6, 7), (6, 7, 7), (7, 8, 7))
 
 
 def tile_picked_phpq_gelu_p_kernel(tc, x_words, x_scales, w1, w2_words, w2_scales, pos, offs, out):
@@ -29,112 +35,114 @@ def tile_picked_phpq_gelu_p_kernel(tc, x_words, x_scales, w1, w2_words, w2_scale
         held = ctx.enter_context(tc.tile_pool(name="held", bufs=1))
         ring = ctx.enter_context(tc.tile_pool(name="ring", bufs=1))
         reuse = ctx.enter_context(tc.tile_pool(name="reuse", bufs=1))
-        reuse_raw = ctx.enter_context(tc.tile_pool(name="reuse_raw", bufs=1))
         psum = ctx.enter_context(tc.psum_pool(name="psum", bufs=1))
 
         offsets = held.tile([P, S // 16], U16, name="offsets")
         nc.sync.dma_start(offsets[:], offs)
 
-        scale_table = reuse.tile([P, T], U8, name="scale_table", align_bytes=64, offset=0)
+        scale_table = reuse.tile([P, T], U8, name="scale_table", align_bytes=64, offset=TABLE_AT)
         nc.vector.memset(scale_table[:].bitcast(I32), 0)
-        rows_by_parity = x_scales[0].rearrange("(r e) c -> e r c", e=2)
-        for e in range(2):
-            nc.sync.dma_start(scale_table[e:P:16, :].bitcast(I32), rows_by_parity[e].bitcast(I32))
 
         w1_rows = w1.rearrange("(p j) c -> p j c", j=4)
         w1_raw = []
-        for half in range(2):
-            raw = reuse_raw.tile([P, 4, H // 2], F32, name="w1_raw%d" % half, tag="stage%d" % (half + 1))
-            nc.scalar.dma_start(raw[:], w1_rows[:, :, half * (H // 2) : (half + 1) * (H // 2)])
+
+        def load_w1(part):
+            lo, hi = W1_CUTS[part], W1_CUTS[part + 1]
+            raw = held.tile([P, 4, hi - lo], F32, name="w1_raw%d" % part)
+            nc.sync.dma_start(raw[:], w1_rows[:, :, lo:hi])
             w1_raw.append(raw)
+
+        load_w1(0)
+        nc.sync.dma_start(scale_table[0:P:8, :].bitcast(I32), x_scales[0].bitcast(I32))
         word_table = held.tile([P, T], U32, name="word_table", align_bytes=64)
-        nc.scalar.dma_start(word_table[:].bitcast(I32), x_words[0].rearrange("p c r -> p (c r)").bitcast(I32))
+        nc.sync.dma_start(word_table[:].bitcast(I32), x_words[0].rearrange("p c r -> p (c r)").bitcast(I32))
+        load_w1(1)
         pos_rows = pos.rearrange("(p t) j -> p t j", t=4)
         pos_parts = []
 
-        def load_pos(part):
+        def load_pos(part, piece):
             lo, hi = POS_CUTS[part], POS_CUTS[part + 1]
-            piece = reuse_raw.tile([P, 4, hi - lo], F32, name="pos%d" % part, tag="stage%d" % part)
-            nc.scalar.dma_start(piece[:], pos_rows[:, :, lo:hi])
+            nc.sync.dma_start(piece[:], pos_rows[:, :, lo:hi])
             pos_parts.append((lo, hi, piece))
 
-        load_pos(0)
+        for part in range(2):
+            load_pos(part, held.tile([P, 4, POS_CUTS[part + 1] - POS_CUTS[part]], F32, name="pos%d" % part))
 
-        w2_plane = held.tile([P, N], U8, name="w2_plane", align_bytes=64)
-        nc.vector.memset(w2_plane[:].bitcast(I32), 0)
         warm = held.tile([P, 2], F32, name="warm")
         nc.vector.memset(warm[:, 0:1], 0.0)
         nc.scalar.activation(warm[:, 1:2], warm[:, 0:1], GELU)
-        w2_codes = held.tile([P, N], U32, name="w2_codes", align_bytes=64)
-        nc.gpsimd.dma_start(w2_codes[:].bitcast(I32), w2_words[0].rearrange("p c r -> p (c r)").bitcast(I32))
+        w2_plane = held.tile([P, N], U8, name="w2_plane", align_bytes=64)
+        nc.vector.memset(w2_plane[:].bitcast(I32), 0)
         for q in range(4):
             nc.gpsimd.dma_start(w2_plane[32 * q : 32 * q + 4, :].bitcast(I32), w2_scales[0, 4 * q : 4 * q + 4, :].bitcast(I32))
+        x_plane = held.tile([P, S], U8, name="x_plane", align_bytes=64)
+        nc.vector.memset(x_plane[:].bitcast(I32), 0)
 
-        x_planes = []
-        for piece in range(S // SCALE_PIECE):
-            picked = held.tile([P, SCALE_PIECE], U8, name="picked_scales%d" % piece, align_bytes=64)
-            plane = held.tile([P, SCALE_PIECE], U8, name="x_plane%d" % piece, align_bytes=64)
-            cols = slice(piece * SCALE_PIECE // 16, (piece + 1) * SCALE_PIECE // 16)
-            nc.vector.tensor_copy(picked[:], scale_table[:].indirect(offsets[:, cols]))
-            nc.vector.tensor_copy(plane[:].bitcast(I32), picked[:].bitcast(I32))
-            for e in range(2):
-                nc.sync.dma_start(plane[2 + e : P : 32, :].bitcast(I32), picked[16 + e : P : 32, :].bitcast(I32))
-            x_planes.append(plane)
+        picked_scales = held.tile([P, S], U8, name="picked_scales", align_bytes=64)
+        nc.vector.tensor_copy(picked_scales[:], scale_table[:].indirect(offsets[:]))
+        for q in range(4):
+            nc.sync.dma_start(x_plane[32 * q : 32 * q + 4, :].bitcast(I32), picked_scales[32 * q : 32 * q + 32 : 8, :].bitcast(I32))
+        w2_codes = reuse.tile([P, N], U32, name="w2_codes", align_bytes=64, offset=W2_AT)
+        nc.sync.dma_start(w2_codes[:].bitcast(I32), w2_words[0].rearrange("p c r -> p (c r)").bitcast(I32))
+        load_pos(2, reuse.tile([P, 4, S - POS_CUTS[2]], F32, name="pos2", align_bytes=64, offset=POS_AT))
 
-        w1_bf = held.tile([P, 4 * H], BF16, name="w1_bf", align_bytes=64)
-        w1_dealt = w1_bf[:].rearrange("p (t m j) -> p m j t", t=4, j=4)
-        for half in range(2):
-            nc.scalar.copy(w1_dealt[:, half * 64 : (half + 1) * 64], w1_raw[half][:].rearrange("p j (m t) -> p m j t", t=4))
-            load_pos(half + 1)
-        w1_codes = held.tile([P, H], U32, name="w1_codes", align_bytes=64)
-        w1_plane = reuse.tile([P, H], U8, name="w1_plane", align_bytes=64, offset=0)
-        nc.vector.quantize_mx(out=w1_codes[:].bitcast(FP8X4), scales=w1_plane[:], in_=w1_bf[:])
-
-        picked_words = {}
-        hidden = {}
+        picked_words = []
 
         def gather_words(g):
-            words = reuse.tile([P, GATHER], U32, name="picked_words", bufs=2, align_bytes=64, offset=H)
-            nc.vector.tensor_copy(words[:], word_table[:].indirect(offsets[:, g * GATHER // 16 : (g + 1) * GATHER // 16]))
-            picked_words[g] = words
+            words = reuse.tile([P, WORD_CUTS[g + 1] - WORD_CUTS[g]], U32, name="picked_words%d" % g, align_bytes=64, offset=WORDS_AT[g])
+            nc.vector.tensor_copy(words[:], word_table[:].indirect(offsets[:, WORD_CUTS[g] // 16 : WORD_CUTS[g + 1] // 16]))
+            picked_words.append(words)
 
-        starts = [sum(OUT_WIDTHS[:b]) for b in range(len(OUT_WIDTHS))]
+        gather_words(0)
 
-        def block_of(col):
-            return max(b for b in range(len(starts)) if starts[b] <= col)
+        w1_bf = reuse.tile([P, 4 * H], BF16, name="w1_bf", align_bytes=64, offset=CAST_AT)
+        w1_dealt = w1_bf[:].rearrange("p (t m j) -> p m j t", t=4, j=4)
+        for part in range(2):
+            nc.scalar.copy(w1_dealt[:, W1_CUTS[part] // 4 : W1_CUTS[part + 1] // 4], w1_raw[part][:].rearrange("p j (m t) -> p m j t", t=4))
+        w1_codes = held.tile([P, H], U32, name="w1_codes", align_bytes=64)
+        w1_plane = held.tile([P, H], U8, name="w1_plane", align_bytes=64)
+        nc.vector.quantize_mx(out=w1_codes[:].bitcast(FP8X4), scales=w1_plane[:], in_=w1_bf[:])
+        gather_words(1)
+
+        unit_at = [sum(UNITS[:u]) for u in range(len(UNITS) + 1)]
+        hidden = {}
 
         def first_layer(u):
-            col = u * UNIT
-            words = picked_words[col // GATHER][:, col % GATHER : col % GATHER + UNIT]
-            plane = x_planes[col // SCALE_PIECE][:, col % SCALE_PIECE : col % SCALE_PIECE + UNIT]
-            acc = psum.tile([P, 4, UNIT], F32, name="acc", bufs=4)
+            col, width = unit_at[u], UNITS[u]
+            g = 0 if col < WORD_CUTS[1] else 1
+            words = picked_words[g][:, col - WORD_CUTS[g] : col - WORD_CUTS[g] + width]
+            acc = psum.tile([P, 4, width], F32, name="acc", bufs=4)
             for t in range(4):
                 nc.tensor.matmul_mx(
                     out=acc[:, t, :],
                     lhsT=w1_codes[:, t * P : (t + 1) * P].bitcast(FP8X4),
                     lhsT_scale=w1_plane[:, t * P : (t + 1) * P],
                     rhs=words.bitcast(FP8X4),
-                    rhs_scale=plane,
+                    rhs_scale=x_plane[:, col : col + width],
                     start=True,
                     stop=True,
                 )
             lo, hi, piece = [part for part in pos_parts if part[0] <= col < part[1]][0]
-            pre = ring.tile([P, 4, UNIT], F32, name="pre", bufs=4)
-            nc.vector.tensor_tensor(pre[:], acc[:], piece[:, :, col - lo : col - lo + UNIT], ADD)
-            b = block_of(col)
+            pre = ring.tile([P, 4, width], F32, name="pre", bufs=4)
+            nc.vector.tensor_tensor(pre[:], acc[:], piece[:, :, col - lo : col - lo + width], ADD)
+            b = [b for b in range(len(BLOCKS)) if BLOCKS[b][0] <= u < BLOCKS[b][1]][0]
+            first, last = unit_at[BLOCKS[b][0]], unit_at[BLOCKS[b][1]]
             if b not in hidden:
-                hidden[b] = ring.tile([P, 4 * OUT_WIDTHS[b]], BF16, name="hidden", bufs=3, align_bytes=64)
-            at = 4 * (col - starts[b])
+                hidden[b] = ring.tile([P, 4 * (last - first)], BF16, name="hidden%d" % b, align_bytes=64)
+            at = 4 * (col - first)
             nc.scalar.activation(
-                hidden[b][:, at : at + 4 * UNIT].rearrange("p (c i t) -> p c t i", i=4, t=4),
+                hidden[b][:, at : at + 4 * width].rearrange("p (c i t) -> p c t i", i=4, t=4),
                 pre[:].rearrange("p t (c i) -> p c t i", i=4),
                 GELU,
             )
 
+        out_rows = out.rearrange("(m p) j -> p m j", p=P)
+
         def second_layer(b):
-            width = OUT_WIDTHS[b]
-            codes = ring.tile([P, width], U32, name="h_codes", bufs=3, align_bytes=64)
-            plane = ring.tile([P, width], U8, name="h_plane", bufs=3, align_bytes=64)
+            first, last = unit_at[BLOCKS[b][0]], unit_at[BLOCKS[b][1]]
+            width = last - first
+            codes = ring.tile([P, width], U32, name="h_codes%d" % b, align_bytes=64)
+            plane = ring.tile([P, width], U8, name="h_plane%d" % b, align_bytes=64)
             nc.vector.quantize_mx(out=codes[:].bitcast(FP8X4), scales=plane[:], in_=hidden[b][:])
             res = psum.tile([P, 2, width], F32, name="res", bufs=3)
             for m in range(2):
@@ -147,17 +155,15 @@ def tile_picked_phpq_gelu_p_kernel(tc, x_words, x_scales, w1, w2_words, w2_scale
                     start=True,
                     stop=True,
                 )
-            staged = ring.tile([P, 2, width], F32, name="staged", bufs=5)
-            nc.scalar.copy(staged[:], res[:])
-            nc.sync.dma_start(out.rearrange("(m p) j -> p m j", p=P)[:, :, starts[b] : starts[b] + width], staged[:])
+            staged = ring.tile([P, 2, width], F32, name="staged%d" % b)
+            if b in ON_VECTOR:
+                nc.vector.tensor_copy(staged[:], res[:])
+            else:
+                nc.scalar.copy(staged[:], res[:])
+            nc.sync.dma_start(out_rows[:, :, first:last], staged[:])
 
-        done = 0
-        for u in range(S // UNIT):
-            if u * UNIT % GATHER == 0:
-                gather_words(u * UNIT // GATHER)
+        for u in range(len(UNITS)):
             first_layer(u)
-            while done < len(OUT_WIDTHS) and starts[done] + OUT_WIDTHS[done] <= u * UNIT:
-                second_layer(done)
-                done = done + 1
-        for b in range(done, len(OUT_WIDTHS)):
-            second_layer(b)
+            for b in range(len(BLOCKS)):
+                if BLOCKS[b][2] == u:
+                    second_layer(b)

@@ -17,16 +17,16 @@ ADD = mybir.AluOpType.add
 
 P = 128
 WORD_CUTS = (0, 768, S)
-W1_CUTS = (0, 320, H)
-POS_CUTS = (0, 256, 512, S)
+W1_CUTS = (0, 256, H)
+POS_CUTS = (0, 512, S)
 ON_VECTOR = (2,)
 TABLE_AT = 8192
 W2_AT = TABLE_AT + 64
 POS_AT = TABLE_AT + 64 - 8192
 WORDS_AT = (9280, 16384)
 CAST_AT = 16384
-UNITS = (128, 128, 128, 128, 128, 128, 128, 128)
-BLOCKS = ((0, 2, 3), (2, 4, 5), (4, 6, 7), (6, 7, 7), (7, 8, 7))
+UNITS = (128, 128, 128, 128, 128, 128, 128, 64, 64)
+BLOCKS = ((0, 2, 3), (2, 4, 5), (4, 6, 8), (6, 7, 8), (7, 8, 8), (8, 9, 8))
 
 
 def tile_picked_phpq_gelu_p_kernel(tc, x_words, x_scales, w1, w2_words, w2_scales, pos, offs, out):
@@ -65,7 +65,7 @@ def tile_picked_phpq_gelu_p_kernel(tc, x_words, x_scales, w1, w2_words, w2_scale
             nc.sync.dma_start(piece[:], pos_rows[:, :, lo:hi])
             pos_parts.append((lo, hi, piece))
 
-        for part in range(2):
+        for part in range(1):
             load_pos(part, held.tile([P, 4, POS_CUTS[part + 1] - POS_CUTS[part]], F32, name="pos%d" % part))
 
         warm = held.tile([P, 2], F32, name="warm")
@@ -74,7 +74,7 @@ def tile_picked_phpq_gelu_p_kernel(tc, x_words, x_scales, w1, w2_words, w2_scale
         w2_plane = held.tile([P, N], U8, name="w2_plane", align_bytes=64)
         nc.vector.memset(w2_plane[:].bitcast(I32), 0)
         for q in range(4):
-            nc.gpsimd.dma_start(w2_plane[32 * q : 32 * q + 4, :].bitcast(I32), w2_scales[0, 4 * q : 4 * q + 4, :].bitcast(I32))
+            nc.scalar.dma_start(w2_plane[32 * q : 32 * q + 4, :].bitcast(I32), w2_scales[0, 4 * q : 4 * q + 4, :].bitcast(I32))
         x_plane = held.tile([P, S], U8, name="x_plane", align_bytes=64)
         nc.vector.memset(x_plane[:].bitcast(I32), 0)
 
@@ -84,7 +84,7 @@ def tile_picked_phpq_gelu_p_kernel(tc, x_words, x_scales, w1, w2_words, w2_scale
             nc.sync.dma_start(x_plane[32 * q : 32 * q + 4, :].bitcast(I32), picked_scales[32 * q : 32 * q + 32 : 8, :].bitcast(I32))
         w2_codes = reuse.tile([P, N], U32, name="w2_codes", align_bytes=64, offset=W2_AT)
         nc.sync.dma_start(w2_codes[:].bitcast(I32), w2_words[0].rearrange("p c r -> p (c r)").bitcast(I32))
-        load_pos(2, reuse.tile([P, 4, S - POS_CUTS[2]], F32, name="pos2", align_bytes=64, offset=POS_AT))
+        load_pos(1, reuse.tile([P, 4, S - POS_CUTS[1]], F32, name="pos1", align_bytes=64, offset=POS_AT))
 
         picked_words = []
 

@@ -16,17 +16,27 @@ GELU = mybir.ActivationFunctionType.Gelu_apprx_tanh
 ADD = mybir.AluOpType.add
 
 P = 128
+PACK = 4
+GROUP = 16
+UNIT = 128
+
+W1_CUTS = (0, 256, 384, H)
+POS_CUTS = (0, 128, 384, 640, 896, S)
 WORD_CUTS = (0, 768, S)
-W1_CUTS = (0, 256, H)
-POS_CUTS = (0, 512, S)
-ON_VECTOR = (2,)
+BLOCK_CUTS = (0, 256, 512, 640, 768, 896, S)
+LAG = 2
+
+OVERLAP = 64
 TABLE_AT = 8192
-W2_AT = TABLE_AT + 64
-POS_AT = TABLE_AT + 64 - 8192
-WORDS_AT = (9280, 16384)
-CAST_AT = 16384
-UNITS = (128, 128, 128, 128, 128, 128, 128, 64, 64)
-BLOCKS = ((0, 2, 3), (2, 4, 5), (4, 6, 8), (6, 7, 8), (7, 8, 8), (8, 9, 8))
+POS1_AT = TABLE_AT + OVERLAP - PACK * (POS_CUTS[2] - POS_CUTS[1]) * 4
+W2_AT = TABLE_AT + OVERLAP
+POS2_AT = TABLE_AT + T - OVERLAP
+CAST_AT = 20480
+WORDS_AT = (16384, CAST_AT)
+
+
+def part_of(cuts, col):
+    return max(part for part in range(len(cuts) - 1) if cuts[part] <= col)
 
 
 def tile_picked_phpq_gelu_p_kernel(tc, x_words, x_scales, w1, w2_words, w2_scales, pos, offs, out):
@@ -37,115 +47,121 @@ def tile_picked_phpq_gelu_p_kernel(tc, x_words, x_scales, w1, w2_words, w2_scale
         reuse = ctx.enter_context(tc.tile_pool(name="reuse", bufs=1))
         psum = ctx.enter_context(tc.psum_pool(name="psum", bufs=1))
 
-        offsets = held.tile([P, S // 16], U16, name="offsets")
+        offsets = held.tile([P, S // GROUP], U16, name="offsets")
         nc.sync.dma_start(offsets[:], offs)
 
         scale_table = reuse.tile([P, T], U8, name="scale_table", align_bytes=64, offset=TABLE_AT)
         nc.vector.memset(scale_table[:].bitcast(I32), 0)
 
-        w1_rows = w1.rearrange("(p j) c -> p j c", j=4)
+        w1_rows = w1.rearrange("(p j) c -> p j c", j=PACK)
+        pos_rows = pos.rearrange("(p t) j -> p t j", t=PACK)
         w1_raw = []
+        pos_parts = []
 
         def load_w1(part):
             lo, hi = W1_CUTS[part], W1_CUTS[part + 1]
-            raw = held.tile([P, 4, hi - lo], F32, name="w1_raw%d" % part)
+            raw = held.tile([P, PACK, hi - lo], F32, name="w1_raw%d" % part, tag="raw%d" % part)
             nc.sync.dma_start(raw[:], w1_rows[:, :, lo:hi])
             w1_raw.append(raw)
+
+        def load_pos(part, pool, **place):
+            lo, hi = POS_CUTS[part], POS_CUTS[part + 1]
+            piece = pool.tile([P, PACK, hi - lo], F32, name="pos%d" % part, **place)
+            nc.sync.dma_start(piece[:], pos_rows[:, :, lo:hi])
+            pos_parts.append(piece)
 
         load_w1(0)
         nc.sync.dma_start(scale_table[0:P:8, :].bitcast(I32), x_scales[0].bitcast(I32))
         word_table = held.tile([P, T], U32, name="word_table", align_bytes=64)
         nc.sync.dma_start(word_table[:].bitcast(I32), x_words[0].rearrange("p c r -> p (c r)").bitcast(I32))
         load_w1(1)
-        pos_rows = pos.rearrange("(p t) j -> p t j", t=4)
-        pos_parts = []
-
-        def load_pos(part, piece):
-            lo, hi = POS_CUTS[part], POS_CUTS[part + 1]
-            nc.sync.dma_start(piece[:], pos_rows[:, :, lo:hi])
-            pos_parts.append((lo, hi, piece))
-
-        for part in range(1):
-            load_pos(part, held.tile([P, 4, POS_CUTS[part + 1] - POS_CUTS[part]], F32, name="pos%d" % part))
+        load_w1(2)
+        load_pos(0, held)
 
         warm = held.tile([P, 2], F32, name="warm")
         nc.vector.memset(warm[:, 0:1], 0.0)
         nc.scalar.activation(warm[:, 1:2], warm[:, 0:1], GELU)
+
         w2_plane = held.tile([P, N], U8, name="w2_plane", align_bytes=64)
         nc.vector.memset(w2_plane[:].bitcast(I32), 0)
         for q in range(4):
             nc.scalar.dma_start(w2_plane[32 * q : 32 * q + 4, :].bitcast(I32), w2_scales[0, 4 * q : 4 * q + 4, :].bitcast(I32))
+
         x_plane = held.tile([P, S], U8, name="x_plane", align_bytes=64)
         nc.vector.memset(x_plane[:].bitcast(I32), 0)
-
         picked_scales = held.tile([P, S], U8, name="picked_scales", align_bytes=64)
         nc.vector.tensor_copy(picked_scales[:], scale_table[:].indirect(offsets[:]))
         for q in range(4):
             nc.sync.dma_start(x_plane[32 * q : 32 * q + 4, :].bitcast(I32), picked_scales[32 * q : 32 * q + 32 : 8, :].bitcast(I32))
+        load_pos(1, reuse, align_bytes=64, offset=POS1_AT)
         w2_codes = reuse.tile([P, N], U32, name="w2_codes", align_bytes=64, offset=W2_AT)
         nc.sync.dma_start(w2_codes[:].bitcast(I32), w2_words[0].rearrange("p c r -> p (c r)").bitcast(I32))
-        load_pos(1, reuse.tile([P, 4, S - POS_CUTS[1]], F32, name="pos1", align_bytes=64, offset=POS_AT))
+        load_pos(2, reuse, align_bytes=64, offset=POS2_AT)
 
         picked_words = []
 
-        def gather_words(g):
-            words = reuse.tile([P, WORD_CUTS[g + 1] - WORD_CUTS[g]], U32, name="picked_words%d" % g, align_bytes=64, offset=WORDS_AT[g])
-            nc.vector.tensor_copy(words[:], word_table[:].indirect(offsets[:, WORD_CUTS[g] // 16 : WORD_CUTS[g + 1] // 16]))
+        def gather_words(part):
+            lo, hi = WORD_CUTS[part], WORD_CUTS[part + 1]
+            words = reuse.tile([P, hi - lo], U32, name="picked_words%d" % part, align_bytes=64, offset=WORDS_AT[part])
+            nc.vector.tensor_copy(words[:], word_table[:].indirect(offsets[:, lo // GROUP : hi // GROUP]))
             picked_words.append(words)
 
         gather_words(0)
 
-        w1_bf = reuse.tile([P, 4 * H], BF16, name="w1_bf", align_bytes=64, offset=CAST_AT)
-        w1_dealt = w1_bf[:].rearrange("p (t m j) -> p m j t", t=4, j=4)
-        for part in range(2):
-            nc.scalar.copy(w1_dealt[:, W1_CUTS[part] // 4 : W1_CUTS[part + 1] // 4], w1_raw[part][:].rearrange("p j (m t) -> p m j t", t=4))
+        w1_bf = reuse.tile([P, PACK * H], BF16, name="w1_bf", align_bytes=64, offset=CAST_AT)
+        w1_dealt = w1_bf[:].rearrange("p (t m j) -> p m t j", t=PACK, j=PACK)
+        for part in range(len(W1_CUTS) - 1):
+            m_range = slice(W1_CUTS[part] // PACK, W1_CUTS[part + 1] // PACK)
+            nc.scalar.copy(w1_dealt[:, m_range], w1_raw[part][:].rearrange("p j (m t) -> p m t j", t=PACK))
+        load_pos(3, held, tag="raw1")
+        load_pos(4, held, tag="raw2")
+
         w1_codes = held.tile([P, H], U32, name="w1_codes", align_bytes=64)
         w1_plane = held.tile([P, H], U8, name="w1_plane", align_bytes=64)
-        nc.vector.quantize_mx(out=w1_codes[:].bitcast(FP8X4), scales=w1_plane[:], in_=w1_bf[:])
+        for lo in (0, H // 2):
+            hi = lo + H // 2
+            nc.vector.quantize_mx(out=w1_codes[:, lo:hi].bitcast(FP8X4), scales=w1_plane[:, lo:hi], in_=w1_bf[:, PACK * lo : PACK * hi])
         gather_words(1)
 
-        unit_at = [sum(UNITS[:u]) for u in range(len(UNITS) + 1)]
         hidden = {}
+        results = {}
+        out_rows = out.rearrange("(m p) j -> p m j", p=P)
 
-        def first_layer(u):
-            col, width = unit_at[u], UNITS[u]
-            g = 0 if col < WORD_CUTS[1] else 1
-            words = picked_words[g][:, col - WORD_CUTS[g] : col - WORD_CUTS[g] + width]
-            acc = psum.tile([P, 4, width], F32, name="acc", bufs=4)
-            for t in range(4):
+        def first_layer(col):
+            part = part_of(WORD_CUTS, col)
+            words = picked_words[part][:, col - WORD_CUTS[part] : col - WORD_CUTS[part] + UNIT]
+            acc = psum.tile([P, PACK, UNIT], F32, name="acc", bufs=4)
+            for t in range(PACK):
                 nc.tensor.matmul_mx(
                     out=acc[:, t, :],
                     lhsT=w1_codes[:, t * P : (t + 1) * P].bitcast(FP8X4),
                     lhsT_scale=w1_plane[:, t * P : (t + 1) * P],
                     rhs=words.bitcast(FP8X4),
-                    rhs_scale=x_plane[:, col : col + width],
+                    rhs_scale=x_plane[:, col : col + UNIT],
                     start=True,
                     stop=True,
                 )
-            lo, hi, piece = [part for part in pos_parts if part[0] <= col < part[1]][0]
-            pre = ring.tile([P, 4, width], F32, name="pre", bufs=4)
-            nc.vector.tensor_tensor(pre[:], acc[:], piece[:, :, col - lo : col - lo + width], ADD)
-            b = [b for b in range(len(BLOCKS)) if BLOCKS[b][0] <= u < BLOCKS[b][1]][0]
-            first, last = unit_at[BLOCKS[b][0]], unit_at[BLOCKS[b][1]]
-            if b not in hidden:
-                hidden[b] = ring.tile([P, 4 * (last - first)], BF16, name="hidden%d" % b, align_bytes=64)
-            at = 4 * (col - first)
+            part = part_of(POS_CUTS, col)
+            pre = ring.tile([P, PACK, UNIT], F32, name="pre", bufs=4)
+            nc.vector.tensor_tensor(pre[:], acc[:], pos_parts[part][:, :, col - POS_CUTS[part] : col - POS_CUTS[part] + UNIT], ADD)
+            block = part_of(BLOCK_CUTS, col)
+            first, last = BLOCK_CUTS[block], BLOCK_CUTS[block + 1]
+            if block not in hidden:
+                hidden[block] = ring.tile([P, PACK * (last - first)], BF16, name="hidden%d" % block, align_bytes=64)
+            at = PACK * (col - first)
             nc.scalar.activation(
-                hidden[b][:, at : at + 4 * width].rearrange("p (c i t) -> p c t i", i=4, t=4),
+                hidden[block][:, at : at + PACK * UNIT].rearrange("p (c i t) -> p c t i", i=4, t=PACK),
                 pre[:].rearrange("p t (c i) -> p c t i", i=4),
                 GELU,
             )
 
-        out_rows = out.rearrange("(m p) j -> p m j", p=P)
-
-        def second_layer(b):
-            first, last = unit_at[BLOCKS[b][0]], unit_at[BLOCKS[b][1]]
-            width = last - first
-            codes = ring.tile([P, width], U32, name="h_codes%d" % b, align_bytes=64)
-            plane = ring.tile([P, width], U8, name="h_plane%d" % b, align_bytes=64)
-            nc.vector.quantize_mx(out=codes[:].bitcast(FP8X4), scales=plane[:], in_=hidden[b][:])
-            res = psum.tile([P, 2, width], F32, name="res", bufs=3)
-            for m in range(2):
+        def second_layer(block):
+            width = BLOCK_CUTS[block + 1] - BLOCK_CUTS[block]
+            codes = ring.tile([P, width], U32, name="h_codes%d" % block, align_bytes=64)
+            plane = ring.tile([P, width], U8, name="h_plane%d" % block, align_bytes=64)
+            nc.vector.quantize_mx(out=codes[:].bitcast(FP8X4), scales=plane[:], in_=hidden[block][:])
+            res = psum.tile([P, N // P, width], F32, name="res", bufs=4)
+            for m in range(N // P):
                 nc.tensor.matmul_mx(
                     out=res[:, m, :],
                     lhsT=w2_codes[:, m * P : (m + 1) * P].bitcast(FP8X4),
@@ -155,15 +171,22 @@ def tile_picked_phpq_gelu_p_kernel(tc, x_words, x_scales, w1, w2_words, w2_scale
                     start=True,
                     stop=True,
                 )
-            staged = ring.tile([P, 2, width], F32, name="staged%d" % b)
-            if b in ON_VECTOR:
-                nc.vector.tensor_copy(staged[:], res[:])
+            results[block] = res
+
+        def store(block):
+            first, last = BLOCK_CUTS[block], BLOCK_CUTS[block + 1]
+            staged = ring.tile([P, N // P, last - first], F32, name="staged%d" % block)
+            if block % 2 == 1:
+                nc.vector.tensor_copy(staged[:], results[block][:])
             else:
-                nc.scalar.copy(staged[:], res[:])
+                nc.scalar.copy(staged[:], results[block][:])
             nc.sync.dma_start(out_rows[:, :, first:last], staged[:])
 
-        for u in range(len(UNITS)):
-            first_layer(u)
-            for b in range(len(BLOCKS)):
-                if BLOCKS[b][2] == u:
-                    second_layer(b)
+        last_unit = S // UNIT - 1
+        for unit in range(last_unit + 1):
+            first_layer(unit * UNIT)
+            due = [b for b in range(len(BLOCK_CUTS) - 1) if min(BLOCK_CUTS[b + 1] // UNIT - 1 + LAG, last_unit) == unit]
+            for block in due:
+                second_layer(block)
+            for block in due:
+                store(block)

@@ -109,10 +109,10 @@ def tile_picked_phpq_gelu_p_kernel(tc, x_words, x_scales, w1, w2_words, w2_scale
         gather_words(0)
 
         w1_bf = reuse.tile([P, PACK * H], BF16, name="w1_bf", align_bytes=64, offset=CAST_AT)
-        w1_dealt = w1_bf[:].rearrange("p (t m j) -> p m t j", t=PACK, j=PACK)
+        w1_dealt = w1_bf[:].rearrange("p (u e m j) -> p m u j e", u=2, e=2, j=PACK)
         for part in range(len(W1_CUTS) - 1):
             m_range = slice(W1_CUTS[part] // PACK, W1_CUTS[part + 1] // PACK)
-            nc.scalar.copy(w1_dealt[:, m_range], w1_raw[part][:].rearrange("p j (m t) -> p m t j", t=PACK))
+            nc.scalar.copy(w1_dealt[:, m_range], w1_raw[part][:].rearrange("p j (m u e) -> p m u j e", u=2, e=2))
         load_pos(3, held, tag="raw1")
         load_pos(4, held, tag="raw2")
 
@@ -150,8 +150,8 @@ def tile_picked_phpq_gelu_p_kernel(tc, x_words, x_scales, w1, w2_words, w2_scale
                 hidden[block] = ring.tile([P, PACK * (last - first)], BF16, name="hidden%d" % block, align_bytes=64)
             at = PACK * (col - first)
             nc.scalar.activation(
-                hidden[block][:, at : at + PACK * UNIT].rearrange("p (c i t) -> p c t i", i=4, t=PACK),
-                pre[:].rearrange("p t (c i) -> p c t i", i=4),
+                hidden[block][:, at : at + PACK * UNIT].rearrange("p (c i t) -> p c t i", i=2, t=PACK),
+                pre[:].rearrange("p t (c i) -> p c t i", i=2),
                 GELU,
             )
 

@@ -20,19 +20,17 @@ PACK = 4
 GROUP = 16
 UNIT = 128
 
-W1_CUTS = (0, 256, 384, H)
 POS_CUTS = (0, 128, 384, 640, 896, S)
-WORD_CUTS = (0, 768, S)
+WORD_CUTS = (0, 256, 768, S)
 BLOCK_CUTS = (0, 256, 512, 640, 768, 896, S)
 LAG = 2
 
 OVERLAP = 64
 TABLE_AT = 8192
-POS1_AT = TABLE_AT + OVERLAP - PACK * (POS_CUTS[2] - POS_CUTS[1]) * 4
-W2_AT = TABLE_AT + OVERLAP
-POS2_AT = TABLE_AT + T - OVERLAP
+RAW_AT = 24576
 CAST_AT = 20480
-WORDS_AT = (16384, CAST_AT)
+POS_AT = (TABLE_AT + OVERLAP - 2048, TABLE_AT + T - OVERLAP, RAW_AT, RAW_AT + 4096, CAST_AT)
+WORDS_AT = (16384, 17408, POS_AT[1] + 128)
 
 
 def part_of(cuts, col):
@@ -51,41 +49,37 @@ def tile_picked_phpq_gelu_p_kernel(tc, x_words, x_scales, w1, w2_words, w2_scale
         nc.sync.dma_start(offsets[:], offs)
 
         scale_table = reuse.tile([P, T], U8, name="scale_table", align_bytes=64, offset=TABLE_AT)
-        nc.vector.memset(scale_table[:].bitcast(I32), 0)
+        nc.vector.memset(scale_table[:, : T // 2].bitcast(I32), 0)
+        nc.gpsimd.memset(scale_table[:, T // 2 :].bitcast(I32), 0)
 
         w1_rows = w1.rearrange("(p j) c -> p j c", j=PACK)
         pos_rows = pos.rearrange("(p t) j -> p t j", t=PACK)
-        w1_raw = []
         pos_parts = []
 
-        def load_w1(part):
-            lo, hi = W1_CUTS[part], W1_CUTS[part + 1]
-            raw = held.tile([P, PACK, hi - lo], F32, name="w1_raw%d" % part, tag="raw%d" % part)
-            nc.sync.dma_start(raw[:], w1_rows[:, :, lo:hi])
-            w1_raw.append(raw)
-
-        def load_pos(part, pool, **place):
+        def load_pos(part):
             lo, hi = POS_CUTS[part], POS_CUTS[part + 1]
-            piece = pool.tile([P, PACK, hi - lo], F32, name="pos%d" % part, **place)
+            piece = reuse.tile([P, PACK, hi - lo], F32, name="pos%d" % part, align_bytes=64, offset=POS_AT[part])
             nc.sync.dma_start(piece[:], pos_rows[:, :, lo:hi])
             pos_parts.append(piece)
 
-        load_w1(0)
+        w1_raw = reuse.tile([P, PACK, H], F32, name="w1_raw", align_bytes=64, offset=RAW_AT)
+        nc.sync.dma_start(w1_raw[:, 0:1], w1_rows[:, 0:1])
         nc.sync.dma_start(scale_table[0:P:8, :].bitcast(I32), x_scales[0].bitcast(I32))
+        nc.sync.dma_start(w1_raw[:, 1:PACK], w1_rows[:, 1:PACK])
+        w2_plane = held.tile([P, N], U8, name="w2_plane", align_bytes=64)
+        nc.vector.memset(w2_plane[:].bitcast(I32), 0)
+        for q in range(4):
+            nc.sync.dma_start(w2_plane[32 * q : 32 * q + 4, :].bitcast(I32), w2_scales[0, 4 * q : 4 * q + 4, :].bitcast(I32))
         word_table = held.tile([P, T], U32, name="word_table", align_bytes=64)
         nc.sync.dma_start(word_table[:].bitcast(I32), x_words[0].rearrange("p c r -> p (c r)").bitcast(I32))
-        load_w1(1)
-        load_w1(2)
-        load_pos(0, held)
+
+        w2_codes = held.tile([P, N], U32, name="w2_codes", align_bytes=64)
+        nc.sync.dma_start(w2_codes[:].bitcast(I32), w2_words[0].rearrange("p c r -> p (c r)").bitcast(I32))
 
         warm = held.tile([P, 2], F32, name="warm")
         nc.vector.memset(warm[:, 0:1], 0.0)
         nc.scalar.activation(warm[:, 1:2], warm[:, 0:1], GELU)
 
-        w2_plane = held.tile([P, N], U8, name="w2_plane", align_bytes=64)
-        nc.vector.memset(w2_plane[:].bitcast(I32), 0)
-        for q in range(4):
-            nc.scalar.dma_start(w2_plane[32 * q : 32 * q + 4, :].bitcast(I32), w2_scales[0, 4 * q : 4 * q + 4, :].bitcast(I32))
 
         x_plane = held.tile([P, S], U8, name="x_plane", align_bytes=64)
         nc.vector.memset(x_plane[:].bitcast(I32), 0)
@@ -93,10 +87,8 @@ def tile_picked_phpq_gelu_p_kernel(tc, x_words, x_scales, w1, w2_words, w2_scale
         nc.vector.tensor_copy(picked_scales[:], scale_table[:].indirect(offsets[:]))
         for q in range(4):
             nc.sync.dma_start(x_plane[32 * q : 32 * q + 4, :].bitcast(I32), picked_scales[32 * q : 32 * q + 32 : 8, :].bitcast(I32))
-        load_pos(1, reuse, align_bytes=64, offset=POS1_AT)
-        w2_codes = reuse.tile([P, N], U32, name="w2_codes", align_bytes=64, offset=W2_AT)
-        nc.sync.dma_start(w2_codes[:].bitcast(I32), w2_words[0].rearrange("p c r -> p (c r)").bitcast(I32))
-        load_pos(2, reuse, align_bytes=64, offset=POS2_AT)
+        load_pos(0)
+        load_pos(1)
 
         picked_words = []
 
@@ -106,21 +98,22 @@ def tile_picked_phpq_gelu_p_kernel(tc, x_words, x_scales, w1, w2_words, w2_scale
             nc.vector.tensor_copy(words[:], word_table[:].indirect(offsets[:, lo // GROUP : hi // GROUP]))
             picked_words.append(words)
 
-        gather_words(0)
 
         w1_bf = reuse.tile([P, PACK * H], BF16, name="w1_bf", align_bytes=64, offset=CAST_AT)
-        w1_dealt = w1_bf[:].rearrange("p (u e m j) -> p m u j e", u=2, e=2, j=PACK)
-        for part in range(len(W1_CUTS) - 1):
-            m_range = slice(W1_CUTS[part] // PACK, W1_CUTS[part + 1] // PACK)
-            nc.scalar.copy(w1_dealt[:, m_range], w1_raw[part][:].rearrange("p j (m u e) -> p m u j e", u=2, e=2))
-        load_pos(3, held, tag="raw1")
-        load_pos(4, held, tag="raw2")
+        w1_dealt = w1_bf[:].rearrange("p (u e m j) -> p u m j e", u=2, e=2, j=PACK)
+        w1_pairs = w1_raw[:].rearrange("p j (m u e) -> p u m j e", u=2, e=2)
+        nc.vector.tensor_copy(w1_dealt[:, 0], w1_pairs[:, 0])
+        nc.scalar.copy(w1_dealt[:, 1], w1_pairs[:, 1])
+        load_pos(2)
+        load_pos(3)
 
         w1_codes = held.tile([P, H], U32, name="w1_codes", align_bytes=64)
         w1_plane = held.tile([P, H], U8, name="w1_plane", align_bytes=64)
         for lo in (0, H // 2):
             hi = lo + H // 2
             nc.vector.quantize_mx(out=w1_codes[:, lo:hi].bitcast(FP8X4), scales=w1_plane[:, lo:hi], in_=w1_bf[:, PACK * lo : PACK * hi])
+        load_pos(4)
+        gather_words(0)
         gather_words(1)
 
         hidden = {}
@@ -185,6 +178,8 @@ def tile_picked_phpq_gelu_p_kernel(tc, x_words, x_scales, w1, w2_words, w2_scale
         last_unit = S // UNIT - 1
         for unit in range(last_unit + 1):
             first_layer(unit * UNIT)
+            if unit == 2:
+                gather_words(2)
             due = [b for b in range(len(BLOCK_CUTS) - 1) if min(BLOCK_CUTS[b + 1] // UNIT - 1 + LAG, last_unit) == unit]
             for block in due:
                 second_layer(block)

@@ -20,8 +20,8 @@ PACK = 4
 GROUP = 16
 UNIT = 128
 
-POS_CUTS = (0, 128, 384, 640, 896, S)
-WORD_CUTS = (0, 256, 768, S)
+POS_CUTS = (0, 256, 512, 768, S)
+WORD_CUTS = (0, 256, S)
 BLOCK_CUTS = (0, 256, 512, 640, 768, 896, S)
 LAG = 2
 
@@ -29,8 +29,8 @@ OVERLAP = 64
 TABLE_AT = 8192
 RAW_AT = 24576
 CAST_AT = 20480
-POS_AT = (TABLE_AT + OVERLAP - 2048, TABLE_AT + T - OVERLAP, RAW_AT, RAW_AT + 4096, CAST_AT)
-WORDS_AT = (16384, 17408, POS_AT[1] + 128)
+POS_AT = (0, TABLE_AT + T - OVERLAP, RAW_AT, RAW_AT + 4096, CAST_AT)
+WORDS_AT = (16384, 17408)
 
 
 def part_of(cuts, col):
@@ -73,8 +73,7 @@ def tile_picked_phpq_gelu_p_kernel(tc, x_words, x_scales, w1, w2_words, w2_scale
         word_table = held.tile([P, T], U32, name="word_table", align_bytes=64)
         nc.sync.dma_start(word_table[:].bitcast(I32), x_words[0].rearrange("p c r -> p (c r)").bitcast(I32))
 
-        w2_codes = held.tile([P, N], U32, name="w2_codes", align_bytes=64)
-        nc.sync.dma_start(w2_codes[:].bitcast(I32), w2_words[0].rearrange("p c r -> p (c r)").bitcast(I32))
+        load_pos(0)
 
         warm = held.tile([P, 2], F32, name="warm")
         nc.vector.memset(warm[:, 0:1], 0.0)
@@ -87,7 +86,8 @@ def tile_picked_phpq_gelu_p_kernel(tc, x_words, x_scales, w1, w2_words, w2_scale
         nc.vector.tensor_copy(picked_scales[:], scale_table[:].indirect(offsets[:]))
         for q in range(4):
             nc.sync.dma_start(x_plane[32 * q : 32 * q + 4, :].bitcast(I32), picked_scales[32 * q : 32 * q + 32 : 8, :].bitcast(I32))
-        load_pos(0)
+        w2_codes = reuse.tile([P, N], U32, name="w2_codes", align_bytes=64, offset=TABLE_AT + OVERLAP)
+        nc.sync.dma_start(w2_codes[:].bitcast(I32), w2_words[0].rearrange("p c r -> p (c r)").bitcast(I32))
         load_pos(1)
 
         picked_words = []
@@ -112,7 +112,6 @@ def tile_picked_phpq_gelu_p_kernel(tc, x_words, x_scales, w1, w2_words, w2_scale
         for lo in (0, H // 2):
             hi = lo + H // 2
             nc.vector.quantize_mx(out=w1_codes[:, lo:hi].bitcast(FP8X4), scales=w1_plane[:, lo:hi], in_=w1_bf[:, PACK * lo : PACK * hi])
-        load_pos(4)
         gather_words(0)
         gather_words(1)
 
@@ -178,8 +177,6 @@ def tile_picked_phpq_gelu_p_kernel(tc, x_words, x_scales, w1, w2_words, w2_scale
         last_unit = S // UNIT - 1
         for unit in range(last_unit + 1):
             first_layer(unit * UNIT)
-            if unit == 2:
-                gather_words(2)
             due = [b for b in range(len(BLOCK_CUTS) - 1) if min(BLOCK_CUTS[b + 1] // UNIT - 1 + LAG, last_unit) == unit]
             for block in due:
                 second_layer(block)

@@ -17,20 +17,26 @@ ADD = mybir.AluOpType.add
 
 P = 128
 PACK = 4
+QUADS = 4
 GROUP = 16
+PAIR = 2
 UNIT = 128
+POS_PART = 256
 
-POS_CUTS = (0, 256, 512, 768, S)
 WORD_CUTS = (0, 256, S)
 BLOCK_CUTS = (0, 256, 512, 640, 768, 896, S)
+LAST_BLOCK = len(BLOCK_CUTS) - 2
 LAG = 2
+ACC_BANKS, RES_BANKS = 3, 5
+PRE_BUFS = 4
 
 OVERLAP = 64
 TABLE_AT = 8192
-RAW_AT = 24576
+W2_AT = TABLE_AT + OVERLAP
+WORDS_AT = 16384
 CAST_AT = 20480
-POS_AT = (0, TABLE_AT + T - OVERLAP, RAW_AT, RAW_AT + 4096, CAST_AT)
-WORDS_AT = (16384, 17408)
+RAW_AT = 24576
+POS_AT = (0, TABLE_AT + T - OVERLAP, RAW_AT, RAW_AT + PACK * POS_PART * 4)
 
 
 def part_of(cuts, col):
@@ -57,9 +63,8 @@ def tile_picked_phpq_gelu_p_kernel(tc, x_words, x_scales, w1, w2_words, w2_scale
         pos_parts = []
 
         def load_pos(part):
-            lo, hi = POS_CUTS[part], POS_CUTS[part + 1]
-            piece = reuse.tile([P, PACK, hi - lo], F32, name="pos%d" % part, align_bytes=64, offset=POS_AT[part])
-            nc.sync.dma_start(piece[:], pos_rows[:, :, lo:hi])
+            piece = reuse.tile([P, PACK, POS_PART], F32, name="pos%d" % part, align_bytes=64, offset=POS_AT[part])
+            nc.sync.dma_start(piece[:], pos_rows[:, :, part * POS_PART : (part + 1) * POS_PART])
             pos_parts.append(piece)
 
         w1_raw = reuse.tile([P, PACK, H], F32, name="w1_raw", align_bytes=64, offset=RAW_AT)
@@ -68,40 +73,29 @@ def tile_picked_phpq_gelu_p_kernel(tc, x_words, x_scales, w1, w2_words, w2_scale
         nc.sync.dma_start(w1_raw[:, 1:PACK], w1_rows[:, 1:PACK])
         w2_plane = held.tile([P, N], U8, name="w2_plane", align_bytes=64)
         nc.vector.memset(w2_plane[:].bitcast(I32), 0)
-        for q in range(4):
+        for q in range(QUADS):
             nc.sync.dma_start(w2_plane[32 * q : 32 * q + 4, :].bitcast(I32), w2_scales[0, 4 * q : 4 * q + 4, :].bitcast(I32))
         word_table = held.tile([P, T], U32, name="word_table", align_bytes=64)
         nc.sync.dma_start(word_table[:].bitcast(I32), x_words[0].rearrange("p c r -> p (c r)").bitcast(I32))
-
         load_pos(0)
 
         warm = held.tile([P, 2], F32, name="warm")
         nc.vector.memset(warm[:, 0:1], 0.0)
         nc.scalar.activation(warm[:, 1:2], warm[:, 0:1], GELU)
 
-
         x_plane = held.tile([P, S], U8, name="x_plane", align_bytes=64)
         nc.vector.memset(x_plane[:].bitcast(I32), 0)
         picked_scales = held.tile([P, S], U8, name="picked_scales", align_bytes=64)
         nc.vector.tensor_copy(picked_scales[:], scale_table[:].indirect(offsets[:]))
-        for q in range(4):
+        for q in range(QUADS):
             nc.sync.dma_start(x_plane[32 * q : 32 * q + 4, :].bitcast(I32), picked_scales[32 * q : 32 * q + 32 : 8, :].bitcast(I32))
-        w2_codes = reuse.tile([P, N], U32, name="w2_codes", align_bytes=64, offset=TABLE_AT + OVERLAP)
+        w2_codes = reuse.tile([P, N], U32, name="w2_codes", align_bytes=64, offset=W2_AT)
         nc.sync.dma_start(w2_codes[:].bitcast(I32), w2_words[0].rearrange("p c r -> p (c r)").bitcast(I32))
         load_pos(1)
 
-        picked_words = []
-
-        def gather_words(part):
-            lo, hi = WORD_CUTS[part], WORD_CUTS[part + 1]
-            words = reuse.tile([P, hi - lo], U32, name="picked_words%d" % part, align_bytes=64, offset=WORDS_AT[part])
-            nc.vector.tensor_copy(words[:], word_table[:].indirect(offsets[:, lo // GROUP : hi // GROUP]))
-            picked_words.append(words)
-
-
         w1_bf = reuse.tile([P, PACK * H], BF16, name="w1_bf", align_bytes=64, offset=CAST_AT)
-        w1_dealt = w1_bf[:].rearrange("p (u e m j) -> p u m j e", u=2, e=2, j=PACK)
-        w1_pairs = w1_raw[:].rearrange("p j (m u e) -> p u m j e", u=2, e=2)
+        w1_dealt = w1_bf[:].rearrange("p (u e m j) -> p u m j e", u=2, e=PAIR, j=PACK)
+        w1_pairs = w1_raw[:].rearrange("p j (m u e) -> p u m j e", u=2, e=PAIR)
         nc.vector.tensor_copy(w1_dealt[:, 0], w1_pairs[:, 0])
         nc.scalar.copy(w1_dealt[:, 1], w1_pairs[:, 1])
         load_pos(2)
@@ -112,8 +106,13 @@ def tile_picked_phpq_gelu_p_kernel(tc, x_words, x_scales, w1, w2_words, w2_scale
         for lo in (0, H // 2):
             hi = lo + H // 2
             nc.vector.quantize_mx(out=w1_codes[:, lo:hi].bitcast(FP8X4), scales=w1_plane[:, lo:hi], in_=w1_bf[:, PACK * lo : PACK * hi])
-        gather_words(0)
-        gather_words(1)
+
+        picked_words = []
+        for part in range(len(WORD_CUTS) - 1):
+            lo, hi = WORD_CUTS[part], WORD_CUTS[part + 1]
+            picked = reuse.tile([P, hi - lo], U32, name="picked_words%d" % part, align_bytes=64, offset=WORDS_AT + 4 * lo)
+            nc.vector.tensor_copy(picked[:], word_table[:].indirect(offsets[:, lo // GROUP : hi // GROUP]))
+            picked_words.append(picked)
 
         hidden = {}
         results = {}
@@ -122,7 +121,7 @@ def tile_picked_phpq_gelu_p_kernel(tc, x_words, x_scales, w1, w2_words, w2_scale
         def first_layer(col):
             part = part_of(WORD_CUTS, col)
             words = picked_words[part][:, col - WORD_CUTS[part] : col - WORD_CUTS[part] + UNIT]
-            acc = psum.tile([P, PACK, UNIT], F32, name="acc", bufs=4)
+            acc = psum.tile([P, PACK, UNIT], F32, name="acc", bufs=ACC_BANKS)
             for t in range(PACK):
                 nc.tensor.matmul_mx(
                     out=acc[:, t, :],
@@ -133,17 +132,16 @@ def tile_picked_phpq_gelu_p_kernel(tc, x_words, x_scales, w1, w2_words, w2_scale
                     start=True,
                     stop=True,
                 )
-            part = part_of(POS_CUTS, col)
-            pre = ring.tile([P, PACK, UNIT], F32, name="pre", bufs=4)
-            nc.vector.tensor_tensor(pre[:], acc[:], pos_parts[part][:, :, col - POS_CUTS[part] : col - POS_CUTS[part] + UNIT], ADD)
+            pre = ring.tile([P, PACK, UNIT], F32, name="pre", bufs=PRE_BUFS)
+            nc.vector.tensor_tensor(pre[:], acc[:], pos_parts[col // POS_PART][:, :, col % POS_PART : col % POS_PART + UNIT], ADD)
             block = part_of(BLOCK_CUTS, col)
             first, last = BLOCK_CUTS[block], BLOCK_CUTS[block + 1]
             if block not in hidden:
                 hidden[block] = ring.tile([P, PACK * (last - first)], BF16, name="hidden%d" % block, align_bytes=64)
             at = PACK * (col - first)
             nc.scalar.activation(
-                hidden[block][:, at : at + PACK * UNIT].rearrange("p (c i t) -> p c t i", i=2, t=PACK),
-                pre[:].rearrange("p t (c i) -> p c t i", i=2),
+                hidden[block][:, at : at + PACK * UNIT].rearrange("p (c i t) -> p c t i", i=PAIR, t=PACK),
+                pre[:].rearrange("p t (c i) -> p c t i", i=PAIR),
                 GELU,
             )
 
@@ -152,10 +150,16 @@ def tile_picked_phpq_gelu_p_kernel(tc, x_words, x_scales, w1, w2_words, w2_scale
             codes = ring.tile([P, width], U32, name="h_codes%d" % block, align_bytes=64)
             plane = ring.tile([P, width], U8, name="h_plane%d" % block, align_bytes=64)
             nc.vector.quantize_mx(out=codes[:].bitcast(FP8X4), scales=plane[:], in_=hidden[block][:])
-            res = psum.tile([P, N // P, width], F32, name="res", bufs=4)
+            if block == LAST_BLOCK:
+                row_tiles = [psum.tile([P, width], F32, name="res_last%d" % m, tag="res", bufs=RES_BANKS)[:] for m in range(N // P)]
+                results[block] = row_tiles
+            else:
+                res = psum.tile([P, N // P, width], F32, name="res", bufs=RES_BANKS)
+                row_tiles = [res[:, m, :] for m in range(N // P)]
+                results[block] = res[:]
             for m in range(N // P):
                 nc.tensor.matmul_mx(
-                    out=res[:, m, :],
+                    out=row_tiles[m],
                     lhsT=w2_codes[:, m * P : (m + 1) * P].bitcast(FP8X4),
                     lhsT_scale=w2_plane[:, m * P : (m + 1) * P],
                     rhs=codes[:].bitcast(FP8X4),
@@ -163,21 +167,23 @@ def tile_picked_phpq_gelu_p_kernel(tc, x_words, x_scales, w1, w2_words, w2_scale
                     start=True,
                     stop=True,
                 )
-            results[block] = res
 
         def store(block):
             first, last = BLOCK_CUTS[block], BLOCK_CUTS[block + 1]
             staged = ring.tile([P, N // P, last - first], F32, name="staged%d" % block)
-            if block % 2 == 1:
-                nc.vector.tensor_copy(staged[:], results[block][:])
+            if block == LAST_BLOCK:
+                nc.vector.tensor_copy(staged[:, 0, :], results[block][0])
+                nc.scalar.copy(staged[:, 1, :], results[block][1])
+            elif block % 2 == 1:
+                nc.vector.tensor_copy(staged[:], results[block])
             else:
-                nc.scalar.copy(staged[:], results[block][:])
+                nc.scalar.copy(staged[:], results[block])
             nc.sync.dma_start(out_rows[:, :, first:last], staged[:])
 
         last_unit = S // UNIT - 1
         for unit in range(last_unit + 1):
             first_layer(unit * UNIT)
-            due = [b for b in range(len(BLOCK_CUTS) - 1) if min(BLOCK_CUTS[b + 1] // UNIT - 1 + LAG, last_unit) == unit]
+            due = [b for b in range(LAST_BLOCK + 1) if min(BLOCK_CUTS[b + 1] // UNIT - 1 + LAG, last_unit) == unit]
             for block in due:
                 second_layer(block)
             for block in due:

@@ -24,11 +24,11 @@ UNIT = 128
 POS_PART = 256
 
 WORD_CUTS = (0, 256, S)
-BLOCK_CUTS = (0, 256, 512, 640, 768, 896, S)
+BLOCK_CUTS = tuple(range(0, S + 1, UNIT))
+STORE_CUTS = (0, 256, 512, 640, 768, 896, S)
 LAST_BLOCK = len(BLOCK_CUTS) - 2
 LAG = 2
 ACC_BANKS, RES_BANKS = 3, 5
-PRE_BUFS = 4
 
 OVERLAP = 64
 TABLE_AT = 8192
@@ -37,6 +37,14 @@ WORDS_AT = 16384
 CAST_AT = 20480
 RAW_AT = 24576
 POS_AT = (0, TABLE_AT + T - OVERLAP, RAW_AT, RAW_AT + PACK * POS_PART * 4)
+PRE_AT = 40960
+PRE_SLOT = 6144
+PRE_BYTES = PACK * UNIT * 4
+SPARE_AT = PRE_AT + 8 * PRE_SLOT
+
+
+def pre_at(unit):
+    return PRE_AT + unit * PRE_SLOT
 
 
 def part_of(cuts, col):
@@ -132,7 +140,7 @@ def tile_picked_phpq_gelu_p_kernel(tc, x_words, x_scales, w1, w2_words, w2_scale
                     start=True,
                     stop=True,
                 )
-            pre = ring.tile([P, PACK, UNIT], F32, name="pre", bufs=PRE_BUFS)
+            pre = reuse.tile([P, PACK, UNIT], F32, name="pre%d" % col, align_bytes=64, offset=pre_at(col // UNIT))
             nc.vector.tensor_tensor(pre[:], acc[:], pos_parts[col // POS_PART][:, :, col % POS_PART : col % POS_PART + UNIT], ADD)
             block = part_of(BLOCK_CUTS, col)
             first, last = BLOCK_CUTS[block], BLOCK_CUTS[block + 1]
@@ -147,7 +155,8 @@ def tile_picked_phpq_gelu_p_kernel(tc, x_words, x_scales, w1, w2_words, w2_scale
 
         def second_layer(block):
             width = BLOCK_CUTS[block + 1] - BLOCK_CUTS[block]
-            codes = ring.tile([P, width], U32, name="h_codes%d" % block, align_bytes=64)
+            at = pre_at(block + 1) if block < 6 else SPARE_AT + block * 1024
+            codes = reuse.tile([P, width], U32, name="h_codes%d" % block, align_bytes=64, offset=at)
             plane = ring.tile([P, width], U8, name="h_plane%d" % block, align_bytes=64)
             nc.vector.quantize_mx(out=codes[:].bitcast(FP8X4), scales=plane[:], in_=hidden[block][:])
             if block == LAST_BLOCK:
@@ -168,23 +177,31 @@ def tile_picked_phpq_gelu_p_kernel(tc, x_words, x_scales, w1, w2_words, w2_scale
                     stop=True,
                 )
 
+        staged = {}
+
         def store(block):
             first, last = BLOCK_CUTS[block], BLOCK_CUTS[block + 1]
-            staged = ring.tile([P, N // P, last - first], F32, name="staged%d" % block)
+            part = part_of(STORE_CUTS, first)
+            lo, hi = STORE_CUTS[part], STORE_CUTS[part + 1]
+            if part not in staged:
+                at = {0: pre_at(3) + PRE_BYTES - OVERLAP, 1: pre_at(5) + PRE_BYTES - OVERLAP, 2: POS_AT[3], 4: pre_at(7)}.get(part, SPARE_AT + 8192 + part * 1024)
+                staged[part] = reuse.tile([P, N // P, hi - lo], F32, name="staged%d" % part, align_bytes=64, offset=at)
+            rows = staged[part][:, :, first - lo : last - lo]
             if block == LAST_BLOCK:
-                nc.vector.tensor_copy(staged[:, 0, :], results[block][0])
-                nc.scalar.copy(staged[:, 1, :], results[block][1])
-            elif block % 2 == 1:
-                nc.vector.tensor_copy(staged[:], results[block])
+                nc.vector.tensor_copy(rows[:, 0, :], results[block][0])
+                nc.scalar.copy(rows[:, 1, :], results[block][1])
+            elif block in (4, 5):
+                nc.vector.tensor_copy(rows, results[block])
             else:
-                nc.scalar.copy(staged[:], results[block])
-            nc.sync.dma_start(out_rows[:, :, first:last], staged[:])
+                nc.scalar.copy(rows, results[block])
+            if last == hi:
+                nc.sync.dma_start(out_rows[:, :, lo:hi], staged[part][:])
 
-        last_unit = S // UNIT - 1
-        for unit in range(last_unit + 1):
-            first_layer(unit * UNIT)
-            due = [b for b in range(LAST_BLOCK + 1) if min(BLOCK_CUTS[b + 1] // UNIT - 1 + LAG, last_unit) == unit]
-            for block in due:
-                second_layer(block)
-            for block in due:
-                store(block)
+        units = S // UNIT
+        for step in range(units + LAG + 1):
+            if step < units:
+                first_layer(step * UNIT)
+            if 0 <= step - LAG < units:
+                second_layer(step - LAG)
+            if 0 <= step - LAG - 1:
+                store(step - LAG - 1)

@@ -140,8 +140,14 @@ def tile_picked_phpq_gelu_p_kernel(tc, x_words, x_scales, w1, w2_words, w2_scale
                     start=True,
                     stop=True,
                 )
-            pre = reuse.tile([P, PACK, UNIT], F32, name="pre%d" % col, align_bytes=64, offset=pre_at(col // UNIT))
-            nc.vector.tensor_tensor(pre[:], acc[:], pos_parts[col // POS_PART][:, :, col % POS_PART : col % POS_PART + UNIT], ADD)
+            pre = reuse.tile([P, UNIT // PAIR, PACK, PAIR], F32, name="pre%d" % col, align_bytes=64, offset=pre_at(col // UNIT))
+            pos_cols = pos_parts[col // POS_PART][:, :, col % POS_PART : col % POS_PART + UNIT]
+            nc.vector.tensor_tensor(
+                pre[:],
+                acc[:].rearrange("p t (c i) -> p c t i", i=PAIR),
+                pos_cols.rearrange("p t (c i) -> p c t i", i=PAIR),
+                ADD,
+            )
             block = part_of(BLOCK_CUTS, col)
             first, last = BLOCK_CUTS[block], BLOCK_CUTS[block + 1]
             if block not in hidden:
@@ -149,7 +155,7 @@ def tile_picked_phpq_gelu_p_kernel(tc, x_words, x_scales, w1, w2_words, w2_scale
             at = PACK * (col - first)
             nc.scalar.activation(
                 hidden[block][:, at : at + PACK * UNIT].rearrange("p (c i t) -> p c t i", i=PAIR, t=PACK),
-                pre[:].rearrange("p t (c i) -> p c t i", i=PAIR),
+                pre[:],
                 GELU,
             )
 

@@ -36,7 +36,7 @@ W2_AT = TABLE_AT + OVERLAP
 WORDS_AT = 16384
 CAST_AT = 20480
 RAW_AT = 24576
-POS_AT = (0, TABLE_AT + T - OVERLAP, RAW_AT, RAW_AT + PACK * POS_PART * 4)
+POS_AT = (0, TABLE_AT + T - OVERLAP, RAW_AT + 1024, RAW_AT + 1024 + PACK * POS_PART * 4)
 PRE_AT = 40960
 PRE_SLOT = 6144
 PRE_BYTES = PACK * UNIT * 4
@@ -81,10 +81,16 @@ def tile_picked_phpq_gelu_p_kernel(tc, x_words, x_scales, w1, w2_words, w2_scale
         nc.sync.dma_start(w1_raw[:, 1:PACK], w1_rows[:, 1:PACK])
         w2_plane = held.tile([P, N], U8, name="w2_plane", align_bytes=64)
         nc.vector.memset(w2_plane[:].bitcast(I32), 0)
-        for q in range(QUADS):
+
+        def load_w2_scales(q):
             nc.sync.dma_start(w2_plane[32 * q : 32 * q + 4, :].bitcast(I32), w2_scales[0, 4 * q : 4 * q + 4, :].bitcast(I32))
+
+        load_w2_scales(0)
+        load_w2_scales(1)
         word_table = held.tile([P, T], U32, name="word_table", align_bytes=64)
         nc.sync.dma_start(word_table[:].bitcast(I32), x_words[0].rearrange("p c r -> p (c r)").bitcast(I32))
+        load_w2_scales(2)
+        load_w2_scales(3)
         load_pos(0)
 
         warm = held.tile([P, 2], F32, name="warm")
@@ -109,11 +115,13 @@ def tile_picked_phpq_gelu_p_kernel(tc, x_words, x_scales, w1, w2_words, w2_scale
         load_pos(2)
         load_pos(3)
 
-        w1_codes = held.tile([P, H], U32, name="w1_codes", align_bytes=64)
-        w1_plane = held.tile([P, H], U8, name="w1_plane", align_bytes=64)
-        for lo in (0, H // 2):
-            hi = lo + H // 2
-            nc.vector.quantize_mx(out=w1_codes[:, lo:hi].bitcast(FP8X4), scales=w1_plane[:, lo:hi], in_=w1_bf[:, PACK * lo : PACK * hi])
+        w1_codes = [
+            reuse.tile([P, H // 2], U32, name="w1_codes0", align_bytes=64, offset=RAW_AT),
+            held.tile([P, H // 2], U32, name="w1_codes1", align_bytes=64),
+        ]
+        w1_planes = [held.tile([P, H // 2], U8, name="w1_plane%d" % u, align_bytes=64) for u in range(2)]
+        for u in (1, 0):
+            nc.vector.quantize_mx(out=w1_codes[u][:].bitcast(FP8X4), scales=w1_planes[u][:], in_=w1_bf[:, u * PAIR * H : (u + 1) * PAIR * H])
 
         picked_words = []
         for part in range(len(WORD_CUTS) - 1):
@@ -133,8 +141,8 @@ def tile_picked_phpq_gelu_p_kernel(tc, x_words, x_scales, w1, w2_words, w2_scale
             for t in range(PACK):
                 nc.tensor.matmul_mx(
                     out=acc[:, t, :],
-                    lhsT=w1_codes[:, t * P : (t + 1) * P].bitcast(FP8X4),
-                    lhsT_scale=w1_plane[:, t * P : (t + 1) * P],
+                    lhsT=w1_codes[t // PAIR][:, t % PAIR * P : (t % PAIR + 1) * P].bitcast(FP8X4),
+                    lhsT_scale=w1_planes[t // PAIR][:, t % PAIR * P : (t % PAIR + 1) * P],
                     rhs=words.bitcast(FP8X4),
                     rhs_scale=x_plane[:, col : col + UNIT],
                     start=True,

@@ -63,8 +63,7 @@ def tile_picked_phpq_gelu_p_kernel(tc, x_words, x_scales, w1, w2_words, w2_scale
         nc.sync.dma_start(offsets[:], offs)
 
         scale_table = reuse.tile([P, T], U8, name="scale_table", align_bytes=64, offset=TABLE_AT)
-        nc.vector.memset(scale_table[:, : T // 2].bitcast(I32), 0)
-        nc.gpsimd.memset(scale_table[:, T // 2 :].bitcast(I32), 0)
+        nc.vector.memset(scale_table[:].bitcast(I32), 0)
 
         w1_rows = w1.rearrange("(p j) c -> p j c", j=PACK)
         pos_rows = pos.rearrange("(p t) j -> p t j", t=PACK)

@@ -100,8 +100,8 @@ def tile_picked_phpq_gelu_p_kernel(tc, x_words, x_scales, w1, w2_words, w2_scale
         nc.vector.memset(x_plane[:].bitcast(I32), 0)
         picked_scales = held.tile([P, S], U8, name="picked_scales", align_bytes=64)
         nc.vector.tensor_copy(picked_scales[:], scale_table[:].indirect(offsets[:]))
-        for q in range(QUADS):
-            nc.sync.dma_start(x_plane[32 * q : 32 * q + 4, :].bitcast(I32), picked_scales[32 * q : 32 * q + 32 : 8, :].bitcast(I32))
+        for a in range(4):
+            nc.sync.dma_start(x_plane[a:P:32, :].bitcast(I32), picked_scales[8 * a : P : 32, :].bitcast(I32))
         w2_codes = reuse.tile([P, N], U32, name="w2_codes", align_bytes=64, offset=W2_AT)
         nc.sync.dma_start(w2_codes[:].bitcast(I32), w2_words[0].rearrange("p c r -> p (c r)").bitcast(I32))
         load_pos(1)
@@ -161,8 +161,8 @@ def tile_picked_phpq_gelu_p_kernel(tc, x_words, x_scales, w1, w2_words, w2_scale
                 hidden[block] = ring.tile([P, PACK * (last - first)], BF16, name="hidden%d" % block, align_bytes=64)
             at = PACK * (col - first)
             nc.scalar.activation(
-                hidden[block][:, at : at + PACK * UNIT].rearrange("p (c i t) -> p c t i", i=PAIR, t=PACK),
-                pre[:],
+                hidden[block][:, at : at + PACK * UNIT].rearrange("p (c i t) -> p c i t", i=PAIR, t=PACK),
+                pre[:].rearrange("p c t i -> p c i t"),
                 GELU,
             )
 

@@ -203,7 +203,7 @@ def tile_picked_phpq_gelu_p_kernel(tc, x_words, x_scales, w1, w2_words, w2_scale
             if block == LAST_BLOCK:
                 nc.vector.tensor_copy(rows[:, 0, :], results[block][0])
                 nc.scalar.copy(rows[:, 1, :], results[block][1])
-            elif block in (4, 5):
+            elif block in (2, 4):
                 nc.vector.tensor_copy(rows, results[block])
             else:
                 nc.scalar.copy(rows, results[block])

@@ -197,7 +197,7 @@ def tile_picked_phpq_gelu_p_kernel(tc, x_words, x_scales, w1, w2_words, w2_scale
             part = part_of(STORE_CUTS, first)
             lo, hi = STORE_CUTS[part], STORE_CUTS[part + 1]
             if part not in staged:
-                at = {0: pre_at(3) + PRE_BYTES - OVERLAP, 1: pre_at(5) + PRE_BYTES - OVERLAP, 2: POS_AT[3], 4: pre_at(7)}.get(part, SPARE_AT + 8192 + part * 1024)
+                at = {0: pre_at(3) + PRE_BYTES - OVERLAP, 1: pre_at(4) + PRE_BYTES - OVERLAP, 2: POS_AT[3], 4: pre_at(7)}.get(part, SPARE_AT + 8192 + part * 1024)
                 staged[part] = reuse.tile([P, N // P, hi - lo], F32, name="staged%d" % part, align_bytes=64, offset=at)
             rows = staged[part][:, :, first - lo : last - lo]
             if block == LAST_BLOCK:

@@ -25,7 +25,7 @@ POS_PART = 256
 
 WORD_CUTS = (0, 256, S)
 BLOCK_CUTS = tuple(range(0, S + 1, UNIT))
-STORE_CUTS = (0, 256, 512, 640, 768, 896, S)
+STORE_CUTS = (0, 384, 512, 640, 768, 896, S)
 LAST_BLOCK = len(BLOCK_CUTS) - 2
 LAG = 2
 ACC_BANKS, RES_BANKS = 3, 5
@@ -147,41 +147,34 @@ def tile_picked_phpq_gelu_p_kernel(tc, x_words, x_scales, w1, w2_words, w2_scale
                     start=True,
                     stop=True,
                 )
-            pre = reuse.tile([P, UNIT // PAIR, PACK, PAIR], F32, name="pre%d" % col, align_bytes=64, offset=pre_at(col // UNIT))
-            pos_cols = pos_parts[col // POS_PART][:, :, col % POS_PART : col % POS_PART + UNIT]
-            nc.vector.tensor_tensor(
-                pre[:],
-                acc[:].rearrange("p t (c i) -> p c t i", i=PAIR),
-                pos_cols.rearrange("p t (c i) -> p c t i", i=PAIR),
-                ADD,
-            )
-            block = part_of(BLOCK_CUTS, col)
-            first, last = BLOCK_CUTS[block], BLOCK_CUTS[block + 1]
-            if block not in hidden:
-                hidden[block] = ring.tile([P, PACK * (last - first)], BF16, name="hidden%d" % block, align_bytes=64)
-            at = PACK * (col - first)
-            nc.scalar.activation(
-                hidden[block][:, at : at + PACK * UNIT].rearrange("p (c i t) -> p c i t", i=PAIR, t=PACK),
-                pre[:].rearrange("p c t i -> p c i t"),
-                GELU,
-            )
+            hidden[col // UNIT] = ring.tile([P, PACK * UNIT], BF16, name="hidden%d" % col, align_bytes=64)
+            width = UNIT // 2 if col == S - UNIT else UNIT
+            for lo in range(0, UNIT, width):
+                pre = reuse.tile([P, width // PAIR, PACK, PAIR], F32, name="pre%d" % (col + lo), align_bytes=64, offset=pre_at(col // UNIT) + PACK * 4 * lo)
+                pos_cols = pos_parts[col // POS_PART][:, :, col % POS_PART + lo : col % POS_PART + lo + width]
+                nc.vector.tensor_tensor(
+                    pre[:],
+                    acc[:, :, lo : lo + width].rearrange("p t (c i) -> p c t i", i=PAIR),
+                    pos_cols.rearrange("p t (c i) -> p c t i", i=PAIR),
+                    ADD,
+                )
+                nc.scalar.activation(
+                    hidden[col // UNIT][:, PACK * lo : PACK * (lo + width)].rearrange("p (c i t) -> p c i t", i=PAIR, t=PACK),
+                    pre[:].rearrange("p c t i -> p c i t"),
+                    GELU,
+                )
 
         def second_layer(block):
             width = BLOCK_CUTS[block + 1] - BLOCK_CUTS[block]
-            at = pre_at(block + 1) if block < 6 else SPARE_AT + block * 1024
+            at = pre_at(block + 1) if block < 5 else SPARE_AT + block * 1024
             codes = reuse.tile([P, width], U32, name="h_codes%d" % block, align_bytes=64, offset=at)
             plane = ring.tile([P, width], U8, name="h_plane%d" % block, align_bytes=64)
             nc.vector.quantize_mx(out=codes[:].bitcast(FP8X4), scales=plane[:], in_=hidden[block][:])
-            if block == LAST_BLOCK:
-                row_tiles = [psum.tile([P, width], F32, name="res_last%d" % m, tag="res", bufs=RES_BANKS)[:] for m in range(N // P)]
-                results[block] = row_tiles
-            else:
-                res = psum.tile([P, N // P, width], F32, name="res", bufs=RES_BANKS)
-                row_tiles = [res[:, m, :] for m in range(N // P)]
-                results[block] = res[:]
+            res = psum.tile([P, N // P, width], F32, name="res", bufs=RES_BANKS)
+            results[block] = res[:]
             for m in range(N // P):
                 nc.tensor.matmul_mx(
-                    out=row_tiles[m],
+                    out=res[:, m, :],
                     lhsT=w2_codes[:, m * P : (m + 1) * P].bitcast(FP8X4),
                     lhsT_scale=w2_plane[:, m * P : (m + 1) * P],
                     rhs=codes[:].bitcast(FP8X4),
@@ -197,13 +190,10 @@ def tile_picked_phpq_gelu_p_kernel(tc, x_words, x_scales, w1, w2_words, w2_scale
             part = part_of(STORE_CUTS, first)
             lo, hi = STORE_CUTS[part], STORE_CUTS[part + 1]
             if part not in staged:
-                at = {0: pre_at(3) + PRE_BYTES - OVERLAP, 1: pre_at(4) + PRE_BYTES - OVERLAP, 2: POS_AT[3], 4: pre_at(7)}.get(part, SPARE_AT + 8192 + part * 1024)
+                at = {0: pre_at(3) + PRE_BYTES - OVERLAP, 1: POS_AT[3], 2: pre_at(7) + PRE_BYTES // 2}.get(part, SPARE_AT + 8192 + part * 1024)
                 staged[part] = reuse.tile([P, N // P, hi - lo], F32, name="staged%d" % part, align_bytes=64, offset=at)
             rows = staged[part][:, :, first - lo : last - lo]
-            if block == LAST_BLOCK:
-                nc.vector.tensor_copy(rows[:, 0, :], results[block][0])
-                nc.scalar.copy(rows[:, 1, :], results[block][1])
-            elif block in (2, 4):
+            if block in (2, 3, LAST_BLOCK):
                 nc.vector.tensor_copy(rows, results[block])
             else:
                 nc.scalar.copy(rows, results[block])
@@ -216,5 +206,6 @@ def tile_picked_phpq_gelu_p_kernel(tc, x_words, x_scales, w1, w2_words, w2_scale
                 first_layer(step * UNIT)
             if 0 <= step - LAG < units:
                 second_layer(step - LAG)
-            if 0 <= step - LAG - 1:
-                store(step - LAG - 1)
+            for block in range(units):
+                if step == (units - 1 if block == 3 else block + LAG + 1):
+                    store(block)

@@ -60,7 +60,6 @@ def tile_picked_phpq_gelu_p_kernel(tc, x_words, x_scales, w1, w2_words, w2_scale
         psum = ctx.enter_context(tc.psum_pool(name="psum", bufs=1))
 
         offsets = held.tile([P, S // GROUP], U16, name="offsets")
-        nc.sync.dma_start(offsets[:], offs)
 
         scale_table = reuse.tile([P, T], U8, name="scale_table", align_bytes=64, offset=TABLE_AT)
         nc.vector.memset(scale_table[:].bitcast(I32), 0)
@@ -76,6 +75,7 @@ def tile_picked_phpq_gelu_p_kernel(tc, x_words, x_scales, w1, w2_words, w2_scale
 
         w1_raw = reuse.tile([P, PACK, H], F32, name="w1_raw", align_bytes=64, offset=RAW_AT)
         nc.sync.dma_start(w1_raw[:, 0:1], w1_rows[:, 0:1])
+        nc.sync.dma_start(offsets[:], offs)
         nc.sync.dma_start(scale_table[0:P:8, :].bitcast(I32), x_scales[0].bitcast(I32))
         nc.sync.dma_start(w1_raw[:, 1:PACK], w1_rows[:, 1:PACK])
         w2_plane = held.tile([P, N], U8, name="w2_plane", align_bytes=64)
@@ -131,6 +131,7 @@ def tile_picked_phpq_gelu_p_kernel(tc, x_words, x_scales, w1, w2_words, w2_scale
 
         hidden = {}
         results = {}
+        whole = {}
         out_rows = out.rearrange("(m p) j -> p m j", p=P)
 
         def first_layer(col):
@@ -171,10 +172,15 @@ def tile_picked_phpq_gelu_p_kernel(tc, x_words, x_scales, w1, w2_words, w2_scale
             plane = ring.tile([P, width], U8, name="h_plane%d" % block, align_bytes=64)
             nc.vector.quantize_mx(out=codes[:].bitcast(FP8X4), scales=plane[:], in_=hidden[block][:])
             res = psum.tile([P, N // P, width], F32, name="res", bufs=RES_BANKS)
-            results[block] = res[:]
+            results[block] = [res[:, m, :] for m in range(N // P)]
+            if block == LAST_BLOCK:
+                spare = psum.tile([P, width], F32, name="acc", bufs=ACC_BANKS)
+                results[block][1] = spare[:]
+            else:
+                whole[block] = res[:]
             for m in range(N // P):
                 nc.tensor.matmul_mx(
-                    out=res[:, m, :],
+                    out=results[block][m],
                     lhsT=w2_codes[:, m * P : (m + 1) * P].bitcast(FP8X4),
                     lhsT_scale=w2_plane[:, m * P : (m + 1) * P],
                     rhs=codes[:].bitcast(FP8X4),
@@ -193,10 +199,13 @@ def tile_picked_phpq_gelu_p_kernel(tc, x_words, x_scales, w1, w2_words, w2_scale
                 at = {0: pre_at(3) + PRE_BYTES - OVERLAP, 1: POS_AT[3], 2: pre_at(7) + PRE_BYTES // 2}.get(part, SPARE_AT + 8192 + part * 1024)
                 staged[part] = reuse.tile([P, N // P, hi - lo], F32, name="staged%d" % part, align_bytes=64, offset=at)
             rows = staged[part][:, :, first - lo : last - lo]
-            if block in (2, 3, LAST_BLOCK):
-                nc.vector.tensor_copy(rows, results[block])
+            if block == LAST_BLOCK:
+                nc.vector.tensor_copy(rows[:, 0, :], results[block][0])
+                nc.scalar.copy(rows[:, 1, :], results[block][1])
+            elif block in (2, 3):
+                nc.vector.tensor_copy(rows, whole[block])
             else:
-                nc.scalar.copy(rows, results[block])
+                nc.scalar.copy(rows, whole[block])
             if last == hi:
                 nc.sync.dma_start(out_rows[:, :, lo:hi], staged[part][:])
 

@@ -24,6 +24,7 @@ UNIT = 128
 POS_PART = 256
 
 WORD_CUTS = (0, 256, S)
+VECTOR_CAST = 96
 BLOCK_CUTS = tuple(range(0, S + 1, UNIT))
 STORE_CUTS = (0, 384, 512, 640, 768, 896, S)
 LAST_BLOCK = len(BLOCK_CUTS) - 2
@@ -109,8 +110,9 @@ def tile_picked_phpq_gelu_p_kernel(tc, x_words, x_scales, w1, w2_words, w2_scale
         w1_bf = reuse.tile([P, PACK * H], BF16, name="w1_bf", align_bytes=64, offset=CAST_AT)
         w1_dealt = w1_bf[:].rearrange("p (u e m j) -> p u m j e", u=2, e=PAIR, j=PACK)
         w1_pairs = w1_raw[:].rearrange("p j (m u e) -> p u m j e", u=2, e=PAIR)
-        nc.vector.tensor_copy(w1_dealt[:, 0], w1_pairs[:, 0])
+        nc.vector.tensor_copy(w1_dealt[:, 0, :VECTOR_CAST], w1_pairs[:, 0, :VECTOR_CAST])
         nc.scalar.copy(w1_dealt[:, 1], w1_pairs[:, 1])
+        nc.scalar.copy(w1_dealt[:, 0, VECTOR_CAST:], w1_pairs[:, 0, VECTOR_CAST:])
         load_pos(2)
         load_pos(3)
 

@@ -25,6 +25,7 @@ POS_PART = 256
 
 WORD_CUTS = (0, 256, S)
 VECTOR_CAST = 96
+EARLY_W1 = 640
 BLOCK_CUTS = tuple(range(0, S + 1, UNIT))
 STORE_CUTS = (0, 384, 512, 640, 768, 896, S)
 LAST_BLOCK = len(BLOCK_CUTS) - 2
@@ -65,7 +66,6 @@ def tile_picked_phpq_gelu_p_kernel(tc, x_words, x_scales, w1, w2_words, w2_scale
         scale_table = reuse.tile([P, T], U8, name="scale_table", align_bytes=64, offset=TABLE_AT)
         nc.vector.memset(scale_table[:].bitcast(I32), 0)
 
-        w1_rows = w1.rearrange("(p j) c -> p j c", j=PACK)
         pos_rows = pos.rearrange("(p t) j -> p t j", t=PACK)
         pos_parts = []
 
@@ -75,10 +75,12 @@ def tile_picked_phpq_gelu_p_kernel(tc, x_words, x_scales, w1, w2_words, w2_scale
             pos_parts.append(piece)
 
         w1_raw = reuse.tile([P, PACK, H], F32, name="w1_raw", align_bytes=64, offset=RAW_AT)
-        nc.sync.dma_start(w1_raw[:, 0:1], w1_rows[:, 0:1])
+        w1_flat = w1_raw[:].rearrange("p j c -> p (j c)")
+        w1_runs = w1.rearrange("(p j) c -> p (j c)", j=PACK)
+        nc.sync.dma_start(w1_flat[:, :EARLY_W1], w1_runs[:, :EARLY_W1])
         nc.sync.dma_start(offsets[:], offs)
         nc.sync.dma_start(scale_table[0:P:8, :].bitcast(I32), x_scales[0].bitcast(I32))
-        nc.sync.dma_start(w1_raw[:, 1:PACK], w1_rows[:, 1:PACK])
+        nc.sync.dma_start(w1_flat[:, EARLY_W1:], w1_runs[:, EARLY_W1:])
         w2_plane = held.tile([P, N], U8, name="w2_plane", align_bytes=64)
         nc.vector.memset(w2_plane[:].bitcast(I32), 0)
 

@@ -27,7 +27,7 @@ WORD_CUTS = (0, 256, S)
 VECTOR_CAST = 96
 EARLY_W1 = 640
 BLOCK_CUTS = tuple(range(0, S + 1, UNIT))
-STORE_CUTS = (0, 384, 512, 640, 768, 896, S)
+STORE_CUTS = (0, 384, 512, 640, 768, S)
 LAST_BLOCK = len(BLOCK_CUTS) - 2
 LAG = 2
 ACC_BANKS, RES_BANKS = 3, 5

from contextlib import ExitStack

import concourse.mybir as mybir

K, T, S, H, N = 512, 2048, 1024, 512, 256
FLOPS = 2 * K * H * S + 2 * H * N * S

F32 = mybir.dt.float32
BF16 = mybir.dt.bfloat16
I32 = mybir.dt.int32
U32 = mybir.dt.uint32
U16 = mybir.dt.uint16
U8 = mybir.dt.uint8
FP8X4 = mybir.dt.float8_e4m3fn_x4
GELU = mybir.ActivationFunctionType.Gelu_apprx_tanh
ADD = mybir.AluOpType.add

P = 128
PACK = 4
QUADS = 4
GROUP = 16
PAIR = 2
UNIT = 128
POS_PART = 256

WORD_CUTS = (0, 256, S)
VECTOR_CAST = 96
EARLY_W1 = 640
BLOCK_CUTS = tuple(range(0, S + 1, UNIT))
STORE_CUTS = (0, 384, 512, 640, 768, S)
LAST_BLOCK = len(BLOCK_CUTS) - 2
LAG = 2
ACC_BANKS, RES_BANKS = 3, 5

OVERLAP = 64
TABLE_AT = 8192
W2_AT = TABLE_AT + OVERLAP
WORDS_AT = 16384
CAST_AT = 20480
RAW_AT = 24576
POS_AT = (0, TABLE_AT + T - OVERLAP, RAW_AT + 1024, RAW_AT + 1024 + PACK * POS_PART * 4)
PRE_AT = 40960
PRE_SLOT = 6144
PRE_BYTES = PACK * UNIT * 4
SPARE_AT = PRE_AT + 8 * PRE_SLOT


def pre_at(unit):
    return PRE_AT + unit * PRE_SLOT


def part_of(cuts, col):
    return max(part for part in range(len(cuts) - 1) if cuts[part] <= col)


def tile_picked_phpq_gelu_p_kernel(tc, x_words, x_scales, w1, w2_words, w2_scales, pos, offs, out):
    nc = tc.nc
    with ExitStack() as ctx:
        held = ctx.enter_context(tc.tile_pool(name="held", bufs=1))
        ring = ctx.enter_context(tc.tile_pool(name="ring", bufs=1))
        reuse = ctx.enter_context(tc.tile_pool(name="reuse", bufs=1))
        psum = ctx.enter_context(tc.psum_pool(name="psum", bufs=1))

        offsets = held.tile([P, S // GROUP], U16, name="offsets")

        scale_table = reuse.tile([P, T], U8, name="scale_table", align_bytes=64, offset=TABLE_AT)
        nc.vector.memset(scale_table[:].bitcast(I32), 0)

        pos_rows = pos.rearrange("(p t) j -> p t j", t=PACK)
        pos_parts = []

        def load_pos(part):
            piece = reuse.tile([P, PACK, POS_PART], F32, name="pos%d" % part, align_bytes=64, offset=POS_AT[part])
            nc.sync.dma_start(piece[:], pos_rows[:, :, part * POS_PART : (part + 1) * POS_PART])
            pos_parts.append(piece)

        w1_raw = reuse.tile([P, PACK, H], F32, name="w1_raw", align_bytes=64, offset=RAW_AT)
        w1_flat = w1_raw[:].rearrange("p j c -> p (j c)")
        w1_runs = w1.rearrange("(p j) c -> p (j c)", j=PACK)
        nc.sync.dma_start(w1_flat[:, :EARLY_W1], w1_runs[:, :EARLY_W1])
        nc.sync.dma_start(offsets[:], offs)
        nc.sync.dma_start(scale_table[0:P:8, :].bitcast(I32), x_scales[0].bitcast(I32))
        nc.sync.dma_start(w1_flat[:, EARLY_W1:], w1_runs[:, EARLY_W1:])
        w2_plane = held.tile([P, N], U8, name="w2_plane", align_bytes=64)
        nc.vector.memset(w2_plane[:].bitcast(I32), 0)

        def load_w2_scales(q):
            nc.sync.dma_start(w2_plane[32 * q : 32 * q + 4, :].bitcast(I32), w2_scales[0, 4 * q : 4 * q + 4, :].bitcast(I32))

        load_w2_scales(0)
        load_w2_scales(1)
        word_table = held.tile([P, T], U32, name="word_table", align_bytes=64)
        nc.sync.dma_start(word_table[:].bitcast(I32), x_words[0].rearrange("p c r -> p (c r)").bitcast(I32))
        load_w2_scales(2)
        load_w2_scales(3)
        load_pos(0)

        warm = held.tile([P, 2], F32, name="warm")
        nc.vector.memset(warm[:, 0:1], 0.0)
        nc.scalar.activation(warm[:, 1:2], warm[:, 0:1], GELU)

        x_plane = held.tile([P, S], U8, name="x_plane", align_bytes=64)
        nc.vector.memset(x_plane[:].bitcast(I32), 0)
        picked_scales = held.tile([P, S], U8, name="picked_scales", align_bytes=64)
        nc.vector.tensor_copy(picked_scales[:], scale_table[:].indirect(offsets[:]))
        for a in range(4):
            nc.sync.dma_start(x_plane[a:P:32, :].bitcast(I32), picked_scales[8 * a : P : 32, :].bitcast(I32))
        w2_codes = reuse.tile([P, N], U32, name="w2_codes", align_bytes=64, offset=W2_AT)
        nc.sync.dma_start(w2_codes[:].bitcast(I32), w2_words[0].rearrange("p c r -> p (c r)").bitcast(I32))
        load_pos(1)

        w1_bf = reuse.tile([P, PACK * H], BF16, name="w1_bf", align_bytes=64, offset=CAST_AT)
        w1_dealt = w1_bf[:].rearrange("p (u e m j) -> p u m j e", u=2, e=PAIR, j=PACK)
        w1_pairs = w1_raw[:].rearrange("p j (m u e) -> p u m j e", u=2, e=PAIR)
        nc.vector.tensor_copy(w1_dealt[:, 0, :VECTOR_CAST], w1_pairs[:, 0, :VECTOR_CAST])
        nc.scalar.copy(w1_dealt[:, 1], w1_pairs[:, 1])
        nc.scalar.copy(w1_dealt[:, 0, VECTOR_CAST:], w1_pairs[:, 0, VECTOR_CAST:])
        load_pos(2)
        load_pos(3)

        w1_codes = [
            reuse.tile([P, H // 2], U32, name="w1_codes0", align_bytes=64, offset=RAW_AT),
            held.tile([P, H // 2], U32, name="w1_codes1", align_bytes=64),
        ]
        w1_planes = [held.tile([P, H // 2], U8, name="w1_plane%d" % u, align_bytes=64) for u in range(2)]
        for u in (1, 0):
            nc.vector.quantize_mx(out=w1_codes[u][:].bitcast(FP8X4), scales=w1_planes[u][:], in_=w1_bf[:, u * PAIR * H : (u + 1) * PAIR * H])

        picked_words = []
        for part in range(len(WORD_CUTS) - 1):
            lo, hi = WORD_CUTS[part], WORD_CUTS[part + 1]
            picked = reuse.tile([P, hi - lo], U32, name="picked_words%d" % part, align_bytes=64, offset=WORDS_AT + 4 * lo)
            nc.vector.tensor_copy(picked[:], word_table[:].indirect(offsets[:, lo // GROUP : hi // GROUP]))
            picked_words.append(picked)

        hidden = {}
        results = {}
        whole = {}
        out_rows = out.rearrange("(m p) j -> p m j", p=P)

        def first_layer(col):
            part = part_of(WORD_CUTS, col)
            words = picked_words[part][:, col - WORD_CUTS[part] : col - WORD_CUTS[part] + UNIT]
            acc = psum.tile([P, PACK, UNIT], F32, name="acc", bufs=ACC_BANKS)
            for t in range(PACK):
                nc.tensor.matmul_mx(
                    out=acc[:, t, :],
                    lhsT=w1_codes[t // PAIR][:, t % PAIR * P : (t % PAIR + 1) * P].bitcast(FP8X4),
                    lhsT_scale=w1_planes[t // PAIR][:, t % PAIR * P : (t % PAIR + 1) * P],
                    rhs=words.bitcast(FP8X4),
                    rhs_scale=x_plane[:, col : col + UNIT],
                    start=True,
                    stop=True,
                )
            hidden[col // UNIT] = ring.tile([P, PACK * UNIT], BF16, name="hidden%d" % col, align_bytes=64)
            width = UNIT // 2 if col == S - UNIT else UNIT
            for lo in range(0, UNIT, width):
                pre = reuse.tile([P, width // PAIR, PACK, PAIR], F32, name="pre%d" % (col + lo), align_bytes=64, offset=pre_at(col // UNIT) + PACK * 4 * lo)
                pos_cols = pos_parts[col // POS_PART][:, :, col % POS_PART + lo : col % POS_PART + lo + width]
                nc.vector.tensor_tensor(
                    pre[:],
                    acc[:, :, lo : lo + width].rearrange("p t (c i) -> p c t i", i=PAIR),
                    pos_cols.rearrange("p t (c i) -> p c t i", i=PAIR),
                    ADD,
                )
                nc.scalar.activation(
                    hidden[col // UNIT][:, PACK * lo : PACK * (lo + width)].rearrange("p (c i t) -> p c i t", i=PAIR, t=PACK),
                    pre[:].rearrange("p c t i -> p c i t"),
                    GELU,
                )

        def second_layer(block):
            width = BLOCK_CUTS[block + 1] - BLOCK_CUTS[block]
            at = pre_at(block + 1) if block < 5 else SPARE_AT + block * 1024
            codes = reuse.tile([P, width], U32, name="h_codes%d" % block, align_bytes=64, offset=at)
            plane = ring.tile([P, width], U8, name="h_plane%d" % block, align_bytes=64)
            nc.vector.quantize_mx(out=codes[:].bitcast(FP8X4), scales=plane[:], in_=hidden[block][:])
            res = psum.tile([P, N // P, width], F32, name="res", bufs=RES_BANKS)
            results[block] = [res[:, m, :] for m in range(N // P)]
            if block == LAST_BLOCK:
                spare = psum.tile([P, width], F32, name="acc", bufs=ACC_BANKS)
                results[block][1] = spare[:]
            else:
                whole[block] = res[:]
            for m in range(N // P):
                nc.tensor.matmul_mx(
                    out=results[block][m],
                    lhsT=w2_codes[:, m * P : (m + 1) * P].bitcast(FP8X4),
                    lhsT_scale=w2_plane[:, m * P : (m + 1) * P],
                    rhs=codes[:].bitcast(FP8X4),
                    rhs_scale=plane[:],
                    start=True,
                    stop=True,
                )

        staged = {}

        def store(block):
            first, last = BLOCK_CUTS[block], BLOCK_CUTS[block + 1]
            part = part_of(STORE_CUTS, first)
            lo, hi = STORE_CUTS[part], STORE_CUTS[part + 1]
            if part not in staged:
                at = {0: pre_at(3) + PRE_BYTES - OVERLAP, 1: POS_AT[3], 2: pre_at(7) + PRE_BYTES // 2}.get(part, SPARE_AT + 8192 + part * 1024)
                staged[part] = reuse.tile([P, N // P, hi - lo], F32, name="staged%d" % part, align_bytes=64, offset=at)
            rows = staged[part][:, :, first - lo : last - lo]
            if block == LAST_BLOCK:
                nc.vector.tensor_copy(rows[:, 0, :], results[block][0])
                nc.scalar.copy(rows[:, 1, :], results[block][1])
            elif block in (2, 3):
                nc.vector.tensor_copy(rows, whole[block])
            else:
                nc.scalar.copy(rows, whole[block])
            if last == hi:
                nc.sync.dma_start(out_rows[:, :, lo:hi], staged[part][:])

        units = S // UNIT
        for step in range(units + LAG + 1):
            if step < units:
                first_layer(step * UNIT)
            if 0 <= step - LAG < units:
                second_layer(step - LAG)
            for block in range(units):
                if step == (units - 1 if block == 3 else block + LAG + 1):
                    store(block)
